import numpy as np
import ml_dtypes


def mxq(x, axis, fmt="e4m3"):
    dtype, down = {"e4m3": (ml_dtypes.float8_e4m3fn, 7), "e5m2": (ml_dtypes.float8_e5m2, 14)}[fmt]
    v = np.moveaxis(np.asarray(x, np.float32).astype(ml_dtypes.bfloat16).astype(np.float64), axis, -1)
    blocks = v.reshape(v.shape[:-1] + (-1, 32))
    amax = np.abs(blocks).max(-1, keepdims=True)
    byte = np.maximum(np.where(amax > 0, np.frexp(amax)[1] - 1 + 127, 0) - down, 1)
    scale = np.exp2(byte - 127.0)
    codes = (blocks / scale).astype(np.float32).astype(dtype).astype(np.float64)
    return np.moveaxis((codes * scale).reshape(v.shape), -1, axis)


WIDE = False


def mx_kscale(k):
    if not WIDE:
        return np.ones(k)
    levels = np.array([10, -10, 5, -5, 0])
    if k % 512:
        return np.exp2(np.random.permutation(np.resize(levels, k // 32))).repeat(32)
    a = np.empty((k // 512, 16))
    for p in range(k // 512):
        a[p, :8] = np.random.permutation(np.resize(levels, 8))
        for g in range(8):
            far = levels[np.abs(levels - a[p, g]) >= 10]
            a[p, g + 8] = far[np.random.randint(len(far))]
    return np.exp2(a.ravel()).repeat(32)


def f64(x):
    return np.asarray(x).astype(np.float64)


def striped(idx):
    return np.tile(idx.reshape(-1, 16).T, (8, 1)).astype(np.uint16)


def unstriped(offs):
    return offs[:16].T.reshape(-1).astype(np.int64)


def pack_weight(w):
    k, n = w.shape
    w = f64(np.asarray(w, np.float32).astype(ml_dtypes.bfloat16)).reshape(k // 32, 32, n)
    amax = np.abs(w).max(1)
    byte = np.clip(np.where(amax > 0, np.frexp(amax)[1] - 1 + 127 - 7, 1), 1, 254)
    scaled = (w * np.exp2(127.0 - byte)[:, None, :]).reshape(k, n).astype(np.float32)
    words = np.ascontiguousarray(scaled.reshape(k // 512, 128, 4, n).transpose(0, 1, 3, 2)).astype(ml_dtypes.float8_e4m3fn).view(np.uint8)
    return words, np.ascontiguousarray(byte.astype(np.uint8).reshape(k // 512, 16, n))


def unpack_weight(words, scales):
    g, p, n, _ = words.shape
    vals = np.ascontiguousarray(words).view(ml_dtypes.float8_e4m3fn).astype(np.float64) * np.repeat(np.exp2(scales.astype(np.float64) - 127.0), 8, axis=1)[..., None]
    return vals.transpose(0, 1, 3, 2).reshape(g * 512, n)


def relu(v):
    return np.maximum(v, 0.0)


K, T, S, V, H, N = 512, 1024, 512, 256, 512, 128


def setup_inputs():
    n = np.random.standard_normal
    s = mx_kscale(K)[:, None]
    u = mx_kscale(H)
    packed_xT = pack_weight(n((K, T)) * s)
    return {
        "x_words": packed_xT[0],
        "x_scales": packed_xT[1],
        "w1": (n((K, H)) / np.sqrt(K) / s * u).astype(np.float32),
        "w2": (n((H, N)) / np.sqrt(2 * H) / u[:, None]).astype(np.float32),
        "w3": (n((H, N)) / np.sqrt(2 * H) / u[:, None]).astype(np.float32),
        "offs": striped(np.random.permutation(T)[:S]),
        "cen": striped(np.random.permutation(S)[:V]),
        "pos1": striped(np.random.permutation(S)[:V]),
        "pos2": striped(np.random.permutation(S)[:V]),
    }


def reference(x_words, x_scales, w1, w2, w3, offs, cen, pos1, pos2):
    xq = unpack_weight(x_words, x_scales)[:, unstriped(offs)]
    h = relu(mxq(f64(w1), 0, "e4m3").T @ xq)
    hc = h[:, unstriped(cen)]
    z = (h[:, unstriped(pos1)] + h[:, unstriped(pos2)]) / 2
    return mxq(f64(w2), 0, "e4m3").T @ mxq(hc, 0, "e4m3") + mxq(f64(w3), 0, "e4m3").T @ mxq(z, 0, "e4m3")

@@ -1,0 +1,153 @@
+from contextlib import ExitStack
+
+import concourse.mybir as mybir
+
+K, T, S, V, H, N = 512, 1024, 512, 256, 512, 128
+FLOPS = 2 * K * S * H + 2 * 2 * H * V * N
+
+F32 = mybir.dt.float32
+BF16 = mybir.dt.bfloat16
+I32 = mybir.dt.int32
+U32 = mybir.dt.uint32
+U16 = mybir.dt.uint16
+U8 = mybir.dt.uint8
+FP8X4 = mybir.dt.float8_e4m3fn_x4
+ACT = mybir.ActivationFunctionType
+ALU = mybir.AluOpType
+
+P = 128
+PACK = 4
+LIST = 16
+HALF = V // 2
+
+
+def tile_picked_sagecat_mean_p_kernel(tc, x_words, x_scales, w1, w2, w3, offs, cen, pos1, pos2, out):
+    nc = tc.nc
+    with ExitStack() as ctx:
+        lists = ctx.enter_context(tc.tile_pool(name="lists", bufs=1))
+        keep = ctx.enter_context(tc.tile_pool(name="keep", bufs=1))
+        psum = ctx.enter_context(tc.psum_pool(name="psum", bufs=1))
+
+        offs_t = lists.tile([P, S // LIST], U16, name="offs_t")
+        cen_t = lists.tile([P, V // LIST], U16, name="cen_t")
+        pos_t = [lists.tile([P, V // LIST], U16, name=f"pos_t{d}") for d in range(2)]
+
+        scale_table = keep.tile([P, T], U8, name="scale_table", align_bytes=64)
+        word_table = keep.tile([P, T], I32, name="word_table", align_bytes=64)
+        nc.vector.memset(scale_table[:].bitcast(I32), 0)
+
+        ones = keep.tile([P, 1], F32, name="ones")
+        half = keep.tile([P, 1], F32, name="half")
+        nc.gpsimd.memset(ones[:], 1.0)
+        nc.scalar.activation(half[:], ones[:], ACT.Relu, scale=0.5)
+
+        w1_rows = w1.rearrange("(p j) c -> p j c", j=PACK)
+        w1_raw = [keep.tile([P, PACK, H // 2], F32, name=f"w1_raw{c}") for c in range(2)]
+        nc.sync.dma_start(w1_raw[0][:], w1_rows[:, :, 0 : H // 2])
+        nc.sync.dma_start(offs_t[:], offs)
+        for q in range(4):
+            nc.sync.dma_start(scale_table[32 * q : 32 * q + 4, :].bitcast(I32), x_scales[0, 4 * q : 4 * q + 4, :].bitcast(I32))
+        nc.sync.dma_start(w1_raw[1][:], w1_rows[:, :, H // 2 : H])
+        nc.sync.dma_start(word_table[:], x_words[0].rearrange("p n t -> p (n t)").bitcast(I32))
+        nc.sync.dma_start(cen_t[:], cen)
+        nc.sync.dma_start(pos_t[0][:], pos1)
+        nc.sync.dma_start(pos_t[1][:], pos2)
+        w2_raw = keep.tile([P, PACK, N], F32, name="w2_raw")
+        w3_raw = keep.tile([P, PACK, N], F32, name="w3_raw")
+        nc.sync.dma_start(w2_raw[:], w2.rearrange("(p j) n -> p j n", j=PACK))
+        nc.sync.dma_start(w3_raw[:], w3.rearrange("(p j) n -> p j n", j=PACK))
+
+        x_scale = keep.tile([P, S], U8, name="x_scale", align_bytes=64)
+        nc.vector.tensor_copy(x_scale[:], scale_table[:].indirect(offs_t[:]))
+
+        w1_bf = keep.tile([P, PACK * P * PACK], BF16, name="w1_bf", align_bytes=64)
+        w1_dst = w1_bf[:].rearrange("p (t m j) -> p m j t", t=PACK, j=PACK)
+        for c, m0, m1, eng in ((0, 0, 32, "s"), (0, 32, 64, "v"), (1, 64, 88, "s"), (1, 88, 128, "v")):
+            src = w1_raw[c][:].rearrange("p j (m t) -> p m j t", t=PACK)[:, m0 - 64 * c : m1 - 64 * c]
+            if eng == "s":
+                nc.scalar.copy(w1_dst[:, m0:m1], src)
+            else:
+                nc.vector.tensor_copy(w1_dst[:, m0:m1], src)
+
+        w1_code = [keep.tile([P, P], U32, name=f"w1_code{t}", align_bytes=64) for t in range(PACK)]
+        w1_scale = [keep.tile([P, P], U8, name=f"w1_scale{t}", align_bytes=64) for t in range(PACK)]
+
+        def quantize_w1(t):
+            nc.vector.quantize_mx(out=w1_code[t][:].bitcast(FP8X4), scales=w1_scale[t][:], in_=w1_bf[:, t * P * PACK : (t + 1) * P * PACK])
+
+        quantize_w1(0)
+        x_code = keep.tile([P, S], U32, name="x_code", align_bytes=64)
+        pieces = ((0, 256), (256, 384), (384, 512))
+        for a, b in pieces:
+            nc.vector.tensor_copy(x_code[:, a:b], word_table[:].bitcast(U32).indirect(offs_t[:, a // LIST : b // LIST]))
+        for t in range(1, PACK):
+            quantize_w1(t)
+
+        h = [keep.tile([P, S], F32, name=f"h{t}") for t in range(PACK)]
+
+        def layer1(t, a, b, tag):
+            acc = psum.tile([P, b - a], F32, name=tag)
+            nc.tensor.matmul_mx(out=acc[:], lhsT=w1_code[t][:].bitcast(FP8X4), lhsT_scale=w1_scale[t][:],
+                                rhs=x_code[:, a:b].bitcast(FP8X4), rhs_scale=x_scale[:, a:b], start=True, stop=True)
+            nc.scalar.activation(h[t][:, a:b], acc[:], ACT.Relu)
+
+        for a, b in pieces:
+            layer1(0, a, b, f"acc0_{a}")
+        for t in range(1, PACK):
+            layer1(t, 0, S, f"acc{t}")
+
+        w23_bf = keep.tile([P, 2 * N * PACK], BF16, name="w23_bf", align_bytes=64)
+        w23_dst = w23_bf[:].rearrange("p (w c i j) -> p w c j i", w=2, i=4, j=PACK)
+        nc.scalar.copy(w23_dst[:, 0], w2_raw[:].rearrange("p j (c i) -> p c j i", i=4))
+        nc.scalar.activation(w23_dst[:, 1], w3_raw[:].rearrange("p j (c i) -> p c j i", i=4), ACT.Copy, scale=half[:])
+        w23_code = keep.tile([P, 2 * N], U32, name="w23_code", align_bytes=64)
+        w23_scale = keep.tile([P, 2 * N], U8, name="w23_scale", align_bytes=64)
+
+        own = keep.tile([P, PACK, V], F32, name="own")
+        nbr = [keep.tile([P, PACK, V], F32, name=f"nbr{d}") for d in range(2)]
+        for t in range(PACK - 1):
+            nc.vector.tensor_copy(own[:, t, :], h[t][:].indirect(cen_t[:]))
+            for d in range(2):
+                nc.vector.tensor_copy(nbr[d][:, t, :], h[t][:].indirect(pos_t[d][:]))
+            if t == 1:
+                nc.vector.quantize_mx(out=w23_code[:].bitcast(FP8X4), scales=w23_scale[:], in_=w23_bf[:])
+        last = PACK - 1
+        nc.vector.tensor_copy(own[:, last, :], h[last][:].indirect(cen_t[:]))
+
+        act_bf = [keep.tile([P, 2 * HALF * PACK], BF16, name=f"act_bf{u}", align_bytes=64) for u in range(2)]
+        act_code = [keep.tile([P, 2 * HALF], U32, name=f"act_code{u}", align_bytes=64) for u in range(2)]
+        act_scale = [keep.tile([P, 2 * HALF], U8, name=f"act_scale{u}", align_bytes=64) for u in range(2)]
+        for u in range(2):
+            nc.scalar.copy(act_bf[u][:, 0 : HALF * PACK].rearrange("p (c i t) -> p c t i", i=4, t=PACK),
+                           own[:, :, u * HALF : (u + 1) * HALF].rearrange("p t (c i) -> p c t i", i=4))
+
+        def gather_last(d, u):
+            nc.vector.tensor_copy(nbr[d][:, last, u * HALF : (u + 1) * HALF],
+                                  h[last][:].indirect(pos_t[d][:, u * HALF // LIST : (u + 1) * HALF // LIST]))
+
+        def add(u):
+            a, b = [nbr[d][:, :, u * HALF : (u + 1) * HALF].rearrange("p t (c i) -> p c t i", i=4) for d in range(2)]
+            nc.vector.tensor_tensor(act_bf[u][:, HALF * PACK :].rearrange("p (c i t) -> p c t i", i=4, t=PACK), a, b, ALU.add)
+
+        def quantize_act(u):
+            nc.vector.quantize_mx(out=act_code[u][:].bitcast(FP8X4), scales=act_scale[u][:], in_=act_bf[u][:])
+
+        gather_last(0, 0)
+        gather_last(1, 0)
+        gather_last(0, 1)
+        add(0)
+        gather_last(1, 1)
+        add(1)
+        quantize_act(0)
+        quantize_act(1)
+
+        for u in range(2):
+            cols = slice(u * HALF, (u + 1) * HALF)
+            acc = psum.tile([P, HALF], F32, name=f"acc_out{u}")
+            nc.tensor.matmul_mx(out=acc[:], lhsT=w23_code[:, 0:N].bitcast(FP8X4), lhsT_scale=w23_scale[:, 0:N],
+                                rhs=act_code[u][:, 0:HALF].bitcast(FP8X4), rhs_scale=act_scale[u][:, 0:HALF], start=True, stop=False)
+            nc.tensor.matmul_mx(out=acc[:], lhsT=w23_code[:, N : 2 * N].bitcast(FP8X4), lhsT_scale=w23_scale[:, N : 2 * N],
+                                rhs=act_code[u][:, HALF:].bitcast(FP8X4), rhs_scale=act_scale[u][:, HALF:], start=False, stop=True)
+            res = keep.tile([P, HALF], F32, name=f"res{u}")
+            nc.scalar.copy(res[:], acc[:])
+            nc.sync.dma_start(out[:, cols], res[:])

@@ -34,35 +34,37 @@ def tile_picked_sagecat_mean_p_kernel(tc, x_words, x_scales, w1, w2, w3, offs, c
 
         scale_table = keep.tile([P, T], U8, name="scale_table", align_bytes=64)
         word_table = keep.tile([P, T], I32, name="word_table", align_bytes=64)
-        nc.vector.memset(scale_table[:].bitcast(I32), 0)
+        x_scale = keep.tile([P, S], U8, name="x_scale", align_bytes=64)
+        nc.vector.memset(x_scale[:].bitcast(I32), 0)
 
         ones = keep.tile([P, 1], F32, name="ones")
         half = keep.tile([P, 1], F32, name="half")
-        nc.gpsimd.memset(ones[:], 1.0)
+        nc.vector.memset(ones[:], 1.0)
         nc.scalar.activation(half[:], ones[:], ACT.Relu, scale=0.5)
 
-        w1_rows = w1.rearrange("(p j) c -> p j c", j=PACK)
-        w1_raw = [keep.tile([P, PACK, H // 2], F32, name=f"w1_raw{c}") for c in range(2)]
-        nc.sync.dma_start(w1_raw[0][:], w1_rows[:, :, 0 : H // 2])
         nc.sync.dma_start(offs_t[:], offs)
-        for q in range(4):
-            nc.sync.dma_start(scale_table[32 * q : 32 * q + 4, :].bitcast(I32), x_scales[0, 4 * q : 4 * q + 4, :].bitcast(I32))
-        nc.sync.dma_start(w1_raw[1][:], w1_rows[:, :, H // 2 : H])
-        nc.sync.dma_start(word_table[:], x_words[0].rearrange("p n t -> p (n t)").bitcast(I32))
+        nc.sync.dma_start(scale_table[:].bitcast(I32), x_scales[0].bitcast(I32).unsqueeze(1).to_broadcast([16, 8, T // 4]))
         nc.sync.dma_start(cen_t[:], cen)
         nc.sync.dma_start(pos_t[0][:], pos1)
+        nc.sync.dma_start(word_table[:], x_words[0].rearrange("p n t -> p (n t)").bitcast(I32))
+        w1_rows = w1.rearrange("(p j) c -> p j c", j=PACK)
+        w1_raw = [keep.tile([P, PACK, H // 2], F32, name=f"w1_raw{c}", tag=f"raw{c}") for c in range(2)]
+        for c in range(2):
+            nc.sync.dma_start(w1_raw[c][:], w1_rows[:, :, c * H // 2 : (c + 1) * H // 2])
         nc.sync.dma_start(pos_t[1][:], pos2)
-        w2_raw = keep.tile([P, PACK, N], F32, name="w2_raw")
-        w3_raw = keep.tile([P, PACK, N], F32, name="w3_raw")
-        nc.sync.dma_start(w2_raw[:], w2.rearrange("(p j) n -> p j n", j=PACK))
-        nc.sync.dma_start(w3_raw[:], w3.rearrange("(p j) n -> p j n", j=PACK))
 
-        x_scale = keep.tile([P, S], U8, name="x_scale", align_bytes=64)
-        nc.vector.tensor_copy(x_scale[:], scale_table[:].indirect(offs_t[:]))
+        picked_scale = keep.tile([P, S], U8, name="picked_scale", align_bytes=64)
+        nc.vector.tensor_copy(picked_scale[:], scale_table[:].indirect(offs_t[:]))
+        for r in range(4):
+            nc.sync.dma_start(x_scale[r:P:32, :].bitcast(I32), picked_scale[8 * r : P : 32, :].bitcast(I32))
+
+        x_code = keep.tile([P, S], U32, name="x_code", align_bytes=64)
+        nc.vector.tensor_copy(x_code[:], word_table[:].bitcast(U32).indirect(offs_t[:]))
+        pieces = ((0, 256), (256, 384), (384, 512))
 
         w1_bf = keep.tile([P, PACK * P * PACK], BF16, name="w1_bf", align_bytes=64)
         w1_dst = w1_bf[:].rearrange("p (t m j) -> p m j t", t=PACK, j=PACK)
-        for c, m0, m1, eng in ((0, 0, 32, "s"), (0, 32, 64, "v"), (1, 64, 88, "s"), (1, 88, 128, "v")):
+        for c, m0, m1, eng in ((0, 0, 32, "s"), (0, 32, 64, "v"), (1, 64, 92, "s"), (1, 92, 128, "v")):
             src = w1_raw[c][:].rearrange("p j (m t) -> p m j t", t=PACK)[:, m0 - 64 * c : m1 - 64 * c]
             if eng == "s":
                 nc.scalar.copy(w1_dst[:, m0:m1], src)
@@ -72,16 +74,16 @@ def tile_picked_sagecat_mean_p_kernel(tc, x_words, x_scales, w1, w2, w3, offs, c
         w1_code = [keep.tile([P, P], U32, name=f"w1_code{t}", align_bytes=64) for t in range(PACK)]
         w1_scale = [keep.tile([P, P], U8, name=f"w1_scale{t}", align_bytes=64) for t in range(PACK)]
 
-        def quantize_w1(t):
-            nc.vector.quantize_mx(out=w1_code[t][:].bitcast(FP8X4), scales=w1_scale[t][:], in_=w1_bf[:, t * P * PACK : (t + 1) * P * PACK])
+        def quantize_w1(t, c):
+            m0, m1 = 64 * c, 64 * (c + 1)
+            nc.vector.quantize_mx(out=w1_code[t][:, m0:m1].bitcast(FP8X4), scales=w1_scale[t][:, m0:m1],
+                                  in_=w1_bf[:, (t * P + m0) * PACK : (t * P + m1) * PACK])
 
-        quantize_w1(0)
-        x_code = keep.tile([P, S], U32, name="x_code", align_bytes=64)
-        pieces = ((0, 256), (256, 384), (384, 512))
-        for a, b in pieces:
-            nc.vector.tensor_copy(x_code[:, a:b], word_table[:].bitcast(U32).indirect(offs_t[:, a // LIST : b // LIST]))
+        for t in range(PACK):
+            quantize_w1(t, 0)
+        quantize_w1(0, 1)
         for t in range(1, PACK):
-            quantize_w1(t)
+            quantize_w1(t, 1)
 
         h = [keep.tile([P, S], F32, name=f"h{t}") for t in range(PACK)]
 
@@ -89,17 +91,25 @@ def tile_picked_sagecat_mean_p_kernel(tc, x_words, x_scales, w1, w2, w3, offs, c
             acc = psum.tile([P, b - a], F32, name=tag)
             nc.tensor.matmul_mx(out=acc[:], lhsT=w1_code[t][:].bitcast(FP8X4), lhsT_scale=w1_scale[t][:],
                                 rhs=x_code[:, a:b].bitcast(FP8X4), rhs_scale=x_scale[:, a:b], start=True, stop=True)
-            nc.scalar.activation(h[t][:, a:b], acc[:], ACT.Relu)
+            if t == 0 and a == 256:
+                nc.vector.tensor_scalar(h[t][:, a:b], acc[:], 0.0, None, ALU.max)
+            else:
+                nc.scalar.activation(h[t][:, a:b], acc[:], ACT.Relu)
 
         for a, b in pieces:
             layer1(0, a, b, f"acc0_{a}")
         for t in range(1, PACK):
             layer1(t, 0, S, f"acc{t}")
 
+        w23_raw = keep.tile([P, 2 * PACK * N], F32, name="w23_raw", tag="raw0")
+        w2_raw = w23_raw[:, 0 : PACK * N]
+        w3_raw = w23_raw[:, PACK * N :]
+        nc.sync.dma_start(w2_raw, w2.rearrange("(p j) n -> p (j n)", j=PACK))
+        nc.sync.dma_start(w3_raw, w3.rearrange("(p j) n -> p (j n)", j=PACK))
         w23_bf = keep.tile([P, 2 * N * PACK], BF16, name="w23_bf", align_bytes=64)
         w23_dst = w23_bf[:].rearrange("p (w c i j) -> p w c j i", w=2, i=4, j=PACK)
-        nc.scalar.copy(w23_dst[:, 0], w2_raw[:].rearrange("p j (c i) -> p c j i", i=4))
-        nc.scalar.activation(w23_dst[:, 1], w3_raw[:].rearrange("p j (c i) -> p c j i", i=4), ACT.Copy, scale=half[:])
+        nc.scalar.copy(w23_dst[:, 0], w2_raw.rearrange("p (j c i) -> p c j i", j=PACK, i=4))
+        nc.scalar.activation(w23_dst[:, 1], w3_raw.rearrange("p (j c i) -> p c j i", j=PACK, i=4), ACT.Copy, scale=half[:])
         w23_code = keep.tile([P, 2 * N], U32, name="w23_code", align_bytes=64)
         w23_scale = keep.tile([P, 2 * N], U8, name="w23_scale", align_bytes=64)
 
@@ -150,4 +160,4 @@ def tile_picked_sagecat_mean_p_kernel(tc, x_words, x_scales, w1, w2, w3, offs, c
                                 rhs=act_code[u][:, HALF:].bitcast(FP8X4), rhs_scale=act_scale[u][:, HALF:], start=False, stop=True)
             res = keep.tile([P, HALF], F32, name=f"res{u}")
             nc.scalar.copy(res[:], acc[:])
-            nc.sync.dma_start(out[:, cols], res[:])
+            (nc.sync, nc.scalar)[u].dma_start(out[:, cols], res[:])

@@ -1,6 +1,7 @@
 from contextlib import ExitStack
 
 import concourse.mybir as mybir
+from concourse.masks import make_identity
 
 K, T, S, V, H, N = 512, 1024, 512, 256, 512, 128
 FLOPS = 2 * K * S * H + 2 * 2 * H * V * N
@@ -34,61 +35,57 @@ def tile_picked_sagecat_mean_p_kernel(tc, x_words, x_scales, w1, w2, w3, offs, c
 
         scale_table = keep.tile([P, T], U8, name="scale_table", align_bytes=64)
         word_table = keep.tile([P, T], I32, name="word_table", align_bytes=64)
-        x_scale = keep.tile([P, S], U8, name="x_scale", align_bytes=64)
-        nc.vector.memset(x_scale[:].bitcast(I32), 0)
+        nc.vector.memset(scale_table[:].bitcast(I32), 0)
 
+        ident = keep.tile([P, P], F32, name="ident")
+        make_identity(nc, ident[:])
         ones = keep.tile([P, 1], F32, name="ones")
         half = keep.tile([P, 1], F32, name="half")
         nc.vector.memset(ones[:], 1.0)
         nc.scalar.activation(half[:], ones[:], ACT.Relu, scale=0.5)
 
-        nc.sync.dma_start(offs_t[:], offs)
-        nc.sync.dma_start(scale_table[:].bitcast(I32), x_scales[0].bitcast(I32).unsqueeze(1).to_broadcast([16, 8, T // 4]))
-        nc.sync.dma_start(cen_t[:], cen)
-        nc.sync.dma_start(pos_t[0][:], pos1)
-        nc.sync.dma_start(word_table[:], x_words[0].rearrange("p n t -> p (n t)").bitcast(I32))
         w1_rows = w1.rearrange("(p j) c -> p j c", j=PACK)
         w1_raw = [keep.tile([P, PACK, H // 2], F32, name=f"w1_raw{c}", tag=f"raw{c}") for c in range(2)]
-        for c in range(2):
-            nc.sync.dma_start(w1_raw[c][:], w1_rows[:, :, c * H // 2 : (c + 1) * H // 2])
+        nc.sync.dma_start(offs_t[:], offs)
+        nc.sync.dma_start(word_table[:], x_words[0].rearrange("p n t -> p (n t)").bitcast(I32))
+        nc.sync.dma_start(w1_raw[0][:], w1_rows[:, :, 0 : H // 2])
+        nc.sync.dma_start(cen_t[:], cen)
+        for q in range(4):
+            nc.sync.dma_start(scale_table[32 * q : 32 * q + 4, :].bitcast(I32), x_scales[0, 4 * q : 4 * q + 4, :].bitcast(I32))
+        nc.sync.dma_start(w1_raw[1][:], w1_rows[:, :, H // 2 : H])
+        nc.sync.dma_start(pos_t[0][:], pos1)
         nc.sync.dma_start(pos_t[1][:], pos2)
 
-        picked_scale = keep.tile([P, S], U8, name="picked_scale", align_bytes=64)
-        nc.vector.tensor_copy(picked_scale[:], scale_table[:].indirect(offs_t[:]))
-        for r in range(4):
-            nc.sync.dma_start(x_scale[r:P:32, :].bitcast(I32), picked_scale[8 * r : P : 32, :].bitcast(I32))
-
         x_code = keep.tile([P, S], U32, name="x_code", align_bytes=64)
+        x_scale = keep.tile([P, S], U8, name="x_scale", align_bytes=64)
         nc.vector.tensor_copy(x_code[:], word_table[:].bitcast(U32).indirect(offs_t[:]))
+        nc.vector.tensor_copy(x_scale[:], scale_table[:].indirect(offs_t[:]))
         pieces = ((0, 256), (256, 384), (384, 512))
 
         w1_bf = keep.tile([P, PACK * P * PACK], BF16, name="w1_bf", align_bytes=64)
         w1_dst = w1_bf[:].rearrange("p (t m j) -> p m j t", t=PACK, j=PACK)
-        for c, m0, m1, eng in ((0, 0, 32, "s"), (0, 32, 64, "v"), (1, 64, 92, "s"), (1, 92, 128, "v")):
+        for c, m0, m1, eng in ((0, 0, 64, "s"), (1, 64, 96, "s"), (1, 96, 128, "v")):
             src = w1_raw[c][:].rearrange("p j (m t) -> p m j t", t=PACK)[:, m0 - 64 * c : m1 - 64 * c]
             if eng == "s":
                 nc.scalar.copy(w1_dst[:, m0:m1], src)
             else:
                 nc.vector.tensor_copy(w1_dst[:, m0:m1], src)
 
-        w1_code = [keep.tile([P, P], U32, name=f"w1_code{t}", align_bytes=64) for t in range(PACK)]
+        w1_code = [keep.tile([P, P], U32, name=f"w1_code{t}", tag=f"code{t}", align_bytes=64) for t in range(PACK)]
         w1_scale = [keep.tile([P, P], U8, name=f"w1_scale{t}", align_bytes=64) for t in range(PACK)]
 
-        def quantize_w1(t, c):
-            m0, m1 = 64 * c, 64 * (c + 1)
+        def quantize_w1(t):
+            m0, m1 = 0, P
             nc.vector.quantize_mx(out=w1_code[t][:, m0:m1].bitcast(FP8X4), scales=w1_scale[t][:, m0:m1],
                                   in_=w1_bf[:, (t * P + m0) * PACK : (t * P + m1) * PACK])
 
         for t in range(PACK):
-            quantize_w1(t, 0)
-        quantize_w1(0, 1)
-        for t in range(1, PACK):
-            quantize_w1(t, 1)
+            quantize_w1(t)
 
         h = [keep.tile([P, S], F32, name=f"h{t}") for t in range(PACK)]
 
         def layer1(t, a, b, tag):
-            acc = psum.tile([P, b - a], F32, name=tag)
+            acc = psum.tile([P, b - a], F32, name="acc", tag=tag)
             nc.tensor.matmul_mx(out=acc[:], lhsT=w1_code[t][:].bitcast(FP8X4), lhsT_scale=w1_scale[t][:],
                                 rhs=x_code[:, a:b].bitcast(FP8X4), rhs_scale=x_scale[:, a:b], start=True, stop=True)
             if t == 0 and a == 256:
@@ -96,10 +93,10 @@ def tile_picked_sagecat_mean_p_kernel(tc, x_words, x_scales, w1, w2, w3, offs, c
             else:
                 nc.scalar.activation(h[t][:, a:b], acc[:], ACT.Relu)
 
-        for a, b in pieces:
-            layer1(0, a, b, f"acc0_{a}")
+        for i, (a, b) in enumerate(pieces):
+            layer1(0, a, b, f"bank{i}")
         for t in range(1, PACK):
-            layer1(t, 0, S, f"acc{t}")
+            layer1(t, 0, S, f"bank{2 + t}")
 
         w23_raw = keep.tile([P, 2 * PACK * N], F32, name="w23_raw", tag="raw0")
         w2_raw = w23_raw[:, 0 : PACK * N]
@@ -113,51 +110,56 @@ def tile_picked_sagecat_mean_p_kernel(tc, x_words, x_scales, w1, w2, w3, offs, c
         w23_code = keep.tile([P, 2 * N], U32, name="w23_code", align_bytes=64)
         w23_scale = keep.tile([P, 2 * N], U8, name="w23_scale", align_bytes=64)
 
-        own = keep.tile([P, PACK, V], F32, name="own")
-        nbr = [keep.tile([P, PACK, V], F32, name=f"nbr{d}") for d in range(2)]
-        for t in range(PACK - 1):
-            nc.vector.tensor_copy(own[:, t, :], h[t][:].indirect(cen_t[:]))
-            for d in range(2):
-                nc.vector.tensor_copy(nbr[d][:, t, :], h[t][:].indirect(pos_t[d][:]))
-            if t == 1:
+        nbr = [keep.tile([P, PACK, V], F32, name=f"nbr{d}", tag=f"nbr{d}") for d in range(2)]
+        sum_t = keep.tile([P, 2 * HALF * PACK], BF16, name="sum_t", tag="code3", align_bytes=64)
+        back = [psum.tile([P, 2, HALF], F32, name="back", tag=f"bank{4 + u}") for u in range(2)]
+        for pair in range(2):
+            turned = [psum.tile([P, 2, P], F32, name="turned", tag=f"bank{2 * pair + u}") for u in range(2)]
+            for e in range(2):
+                t = 2 * pair + e
+                for d in range(2):
+                    nc.vector.tensor_copy(nbr[d][:, t, :], h[t][:].indirect(pos_t[d][:]))
+                    for u in range(2):
+                        nc.tensor.matmul(turned[u][:, e, :], nbr[d][:, t, u * HALF : (u + 1) * HALF], ident[:],
+                                         is_transpose=True, start=(d == 0), stop=(d == 1))
+            for u in range(2):
+                lo = (2 * u + pair) * 2 * P
+                nc.scalar.copy(sum_t[:, lo : lo + 2 * P].rearrange("p (m e) -> p m e", e=2), turned[u][:].rearrange("p e m -> p m e"))
+            for u in range(2):
+                lo = (2 * u + pair) * 2 * P
+                nc.tensor.transpose(back[u][:, pair, :], sum_t[:, lo : lo + 2 * P].bitcast(F32), ident[:])
+            if pair == 0:
                 nc.vector.quantize_mx(out=w23_code[:].bitcast(FP8X4), scales=w23_scale[:], in_=w23_bf[:])
-        last = PACK - 1
-        nc.vector.tensor_copy(own[:, last, :], h[last][:].indirect(cen_t[:]))
 
-        act_bf = [keep.tile([P, 2 * HALF * PACK], BF16, name=f"act_bf{u}", align_bytes=64) for u in range(2)]
-        act_code = [keep.tile([P, 2 * HALF], U32, name=f"act_code{u}", align_bytes=64) for u in range(2)]
-        act_scale = [keep.tile([P, 2 * HALF], U8, name=f"act_scale{u}", align_bytes=64) for u in range(2)]
+        sum_bf = keep.tile([P, V * PACK], BF16, name="sum_bf", align_bytes=64)
         for u in range(2):
-            nc.scalar.copy(act_bf[u][:, 0 : HALF * PACK].rearrange("p (c i t) -> p c t i", i=4, t=PACK),
-                           own[:, :, u * HALF : (u + 1) * HALF].rearrange("p t (c i) -> p c t i", i=4))
+            nc.scalar.copy(sum_bf[:, u * HALF * PACK : (u + 1) * HALF * PACK].bitcast(F32).rearrange("p (v w) -> p v w", w=2),
+                           back[u][:].rearrange("p w v -> p v w"))
 
-        def gather_last(d, u):
-            nc.vector.tensor_copy(nbr[d][:, last, u * HALF : (u + 1) * HALF],
-                                  h[last][:].indirect(pos_t[d][:, u * HALF // LIST : (u + 1) * HALF // LIST]))
+        split = 192
+        own = keep.tile([P, PACK, split], F32, name="own", tag="nbr0")
+        own_bf = keep.tile([P, V * PACK], BF16, name="own_bf", tag="code3", align_bytes=64)
+        for t in range(PACK):
+            nc.vector.tensor_copy(own[:, t, :], h[t][:].indirect(cen_t[:, 0 : split // LIST]))
+        for a, b in ((0, HALF), (HALF, split)):
+            nc.scalar.copy(own_bf[:, a * PACK : b * PACK].rearrange("p (c i t) -> p c t i", i=4, t=PACK),
+                           own[:, :, a:b].rearrange("p t (c i) -> p c t i", i=4))
+        for t in range(PACK):
+            nc.vector.tensor_copy(own_bf[:, split * PACK + t : V * PACK : PACK], h[t][:].indirect(cen_t[:, split // LIST :]))
 
-        def add(u):
-            a, b = [nbr[d][:, :, u * HALF : (u + 1) * HALF].rearrange("p t (c i) -> p c t i", i=4) for d in range(2)]
-            nc.vector.tensor_tensor(act_bf[u][:, HALF * PACK :].rearrange("p (c i t) -> p c t i", i=4, t=PACK), a, b, ALU.add)
-
-        def quantize_act(u):
-            nc.vector.quantize_mx(out=act_code[u][:].bitcast(FP8X4), scales=act_scale[u][:], in_=act_bf[u][:])
-
-        gather_last(0, 0)
-        gather_last(1, 0)
-        gather_last(0, 1)
-        add(0)
-        gather_last(1, 1)
-        add(1)
-        quantize_act(0)
-        quantize_act(1)
-
+        sum_code = keep.tile([P, V], U32, name="sum_code", align_bytes=64)
+        sum_scale = keep.tile([P, V], U8, name="sum_scale", align_bytes=64)
+        nc.vector.quantize_mx(out=sum_code[:].bitcast(FP8X4), scales=sum_scale[:], in_=sum_bf[:])
         for u in range(2):
             cols = slice(u * HALF, (u + 1) * HALF)
+            own_code = keep.tile([P, HALF], U32, name=f"own_code{u}", align_bytes=64)
+            own_scale = keep.tile([P, HALF], U8, name=f"own_scale{u}", align_bytes=64)
+            nc.vector.quantize_mx(out=own_code[:].bitcast(FP8X4), scales=own_scale[:], in_=own_bf[:, u * HALF * PACK : (u + 1) * HALF * PACK])
             acc = psum.tile([P, HALF], F32, name=f"acc_out{u}")
-            nc.tensor.matmul_mx(out=acc[:], lhsT=w23_code[:, 0:N].bitcast(FP8X4), lhsT_scale=w23_scale[:, 0:N],
-                                rhs=act_code[u][:, 0:HALF].bitcast(FP8X4), rhs_scale=act_scale[u][:, 0:HALF], start=True, stop=False)
             nc.tensor.matmul_mx(out=acc[:], lhsT=w23_code[:, N : 2 * N].bitcast(FP8X4), lhsT_scale=w23_scale[:, N : 2 * N],
-                                rhs=act_code[u][:, HALF:].bitcast(FP8X4), rhs_scale=act_scale[u][:, HALF:], start=False, stop=True)
+                                rhs=sum_code[:, cols].bitcast(FP8X4), rhs_scale=sum_scale[:, cols], start=True, stop=False)
+            nc.tensor.matmul_mx(out=acc[:], lhsT=w23_code[:, 0:N].bitcast(FP8X4), lhsT_scale=w23_scale[:, 0:N],
+                                rhs=own_code[:].bitcast(FP8X4), rhs_scale=own_scale[:], start=False, stop=True)
             res = keep.tile([P, HALF], F32, name=f"res{u}")
             nc.scalar.copy(res[:], acc[:])
-            (nc.sync, nc.scalar)[u].dma_start(out[:, cols], res[:])
+            nc.sync.dma_start(out[:, cols], res[:])

@@ -37,21 +37,22 @@ def tile_picked_sagecat_mean_p_kernel(tc, x_words, x_scales, w1, w2, w3, offs, c
         word_table = keep.tile([P, T], I32, name="word_table", align_bytes=64)
         nc.vector.memset(scale_table[:].bitcast(I32), 0)
 
-        ident = keep.tile([P, P], F32, name="ident")
-        make_identity(nc, ident[:])
         ones = keep.tile([P, 1], F32, name="ones")
         half = keep.tile([P, 1], F32, name="half")
         nc.vector.memset(ones[:], 1.0)
+        ident = keep.tile([P, P], F32, name="ident")
+        nc.vector.memset(ident[:], 0.0)
+        make_identity(nc, ident[:], nomemset=True)
         nc.scalar.activation(half[:], ones[:], ACT.Relu, scale=0.5)
 
         w1_rows = w1.rearrange("(p j) c -> p j c", j=PACK)
-        w1_raw = [keep.tile([P, PACK, H // 2], F32, name=f"w1_raw{c}", tag=f"raw{c}") for c in range(2)]
+        w1_raw = [keep.tile([P, PACK, H // 2], F32, name=f"w1_raw{c}") for c in range(2)]
         nc.sync.dma_start(offs_t[:], offs)
         nc.sync.dma_start(word_table[:], x_words[0].rearrange("p n t -> p (n t)").bitcast(I32))
-        nc.sync.dma_start(w1_raw[0][:], w1_rows[:, :, 0 : H // 2])
         nc.sync.dma_start(cen_t[:], cen)
         for q in range(4):
             nc.sync.dma_start(scale_table[32 * q : 32 * q + 4, :].bitcast(I32), x_scales[0, 4 * q : 4 * q + 4, :].bitcast(I32))
+        nc.sync.dma_start(w1_raw[0][:], w1_rows[:, :, 0 : H // 2])
         nc.sync.dma_start(w1_raw[1][:], w1_rows[:, :, H // 2 : H])
         nc.sync.dma_start(pos_t[0][:], pos1)
         nc.sync.dma_start(pos_t[1][:], pos2)
@@ -64,15 +65,13 @@ def tile_picked_sagecat_mean_p_kernel(tc, x_words, x_scales, w1, w2, w3, offs, c
 
         w1_bf = keep.tile([P, PACK * P * PACK], BF16, name="w1_bf", align_bytes=64)
         w1_dst = w1_bf[:].rearrange("p (t m j) -> p m j t", t=PACK, j=PACK)
-        for c, m0, m1, eng in ((0, 0, 64, "s"), (1, 64, 96, "s"), (1, 96, 128, "v")):
-            src = w1_raw[c][:].rearrange("p j (m t) -> p m j t", t=PACK)[:, m0 - 64 * c : m1 - 64 * c]
-            if eng == "s":
-                nc.scalar.copy(w1_dst[:, m0:m1], src)
-            else:
-                nc.vector.tensor_copy(w1_dst[:, m0:m1], src)
+        w1_src = [w1_raw[c][:].rearrange("p j (m t) -> p m j t", t=PACK) for c in range(2)]
+        nc.scalar.copy(w1_dst[:, 0:64], w1_src[0])
+        nc.vector.tensor_copy(w1_dst[:, 64:P, :, 0:2], w1_src[1][:, :, :, 0:2])
+        nc.scalar.copy(w1_dst[:, 64:P, :, 2:4], w1_src[1][:, :, :, 2:4])
 
         w1_code = [keep.tile([P, P], U32, name=f"w1_code{t}", tag=f"code{t}", align_bytes=64) for t in range(PACK)]
-        w1_scale = [keep.tile([P, P], U8, name=f"w1_scale{t}", align_bytes=64) for t in range(PACK)]
+        w1_scale = [keep.tile([P, P], U8, name=f"w1_scale{t}", tag=f"scale{t}", align_bytes=64) for t in range(PACK)]
 
         def quantize_w1(t):
             m0, m1 = 0, P
@@ -98,12 +97,12 @@ def tile_picked_sagecat_mean_p_kernel(tc, x_words, x_scales, w1, w2, w3, offs, c
         for t in range(1, PACK):
             layer1(t, 0, S, f"bank{2 + t}")
 
-        w23_raw = keep.tile([P, 2 * PACK * N], F32, name="w23_raw", tag="raw0")
+        w23_raw = keep.tile([P, 2 * PACK * N], F32, name="w23_raw")
         w2_raw = w23_raw[:, 0 : PACK * N]
         w3_raw = w23_raw[:, PACK * N :]
         nc.sync.dma_start(w2_raw, w2.rearrange("(p j) n -> p (j n)", j=PACK))
         nc.sync.dma_start(w3_raw, w3.rearrange("(p j) n -> p (j n)", j=PACK))
-        w23_bf = keep.tile([P, 2 * N * PACK], BF16, name="w23_bf", align_bytes=64)
+        w23_bf = keep.tile([P, 2 * N * PACK], BF16, name="w23_bf", tag="scale3", align_bytes=64)
         w23_dst = w23_bf[:].rearrange("p (w c i j) -> p w c j i", w=2, i=4, j=PACK)
         nc.scalar.copy(w23_dst[:, 0], w2_raw.rearrange("p (j c i) -> p c j i", j=PACK, i=4))
         nc.scalar.activation(w23_dst[:, 1], w3_raw.rearrange("p (j c i) -> p c j i", j=PACK, i=4), ACT.Copy, scale=half[:])

@@ -18,8 +18,16 @@ ALU = mybir.AluOpType
 
 P = 128
 PACK = 4
+QUADRANT = 32
 LIST = 16
 HALF = V // 2
+RUN = 4
+ALIGN = 64
+
+PLANE0_PIECES = ((0, 256), (256, 384), (384, S))
+PLANE0_PIECE_ON_VECTOR = 1
+
+OWN_SPLIT = 192
 
 
 def tile_picked_sagecat_mean_p_kernel(tc, x_words, x_scales, w1, w2, w3, offs, cen, pos1, pos2, out):
@@ -33,85 +41,88 @@ def tile_picked_sagecat_mean_p_kernel(tc, x_words, x_scales, w1, w2, w3, offs, c
         cen_t = lists.tile([P, V // LIST], U16, name="cen_t")
         pos_t = [lists.tile([P, V // LIST], U16, name=f"pos_t{d}") for d in range(2)]
 
-        scale_table = keep.tile([P, T], U8, name="scale_table", align_bytes=64)
-        word_table = keep.tile([P, T], I32, name="word_table", align_bytes=64)
+        scale_table = keep.tile([P, T], U8, name="scale_table", align_bytes=ALIGN)
+        word_table = keep.tile([P, T], I32, name="word_table", align_bytes=ALIGN)
         nc.vector.memset(scale_table[:].bitcast(I32), 0)
 
-        ones = keep.tile([P, 1], F32, name="ones")
-        half = keep.tile([P, 1], F32, name="half")
-        nc.vector.memset(ones[:], 1.0)
         ident = keep.tile([P, P], F32, name="ident")
         nc.vector.memset(ident[:], 0.0)
         make_identity(nc, ident[:], nomemset=True)
-        nc.scalar.activation(half[:], ones[:], ACT.Relu, scale=0.5)
 
         w1_rows = w1.rearrange("(p j) c -> p j c", j=PACK)
         w1_raw = [keep.tile([P, PACK, H // 2], F32, name=f"w1_raw{c}") for c in range(2)]
         nc.sync.dma_start(offs_t[:], offs)
         nc.sync.dma_start(word_table[:], x_words[0].rearrange("p n t -> p (n t)").bitcast(I32))
         nc.sync.dma_start(cen_t[:], cen)
-        for q in range(4):
-            nc.sync.dma_start(scale_table[32 * q : 32 * q + 4, :].bitcast(I32), x_scales[0, 4 * q : 4 * q + 4, :].bitcast(I32))
+        for q in range(P // QUADRANT):
+            nc.sync.dma_start(
+                scale_table[QUADRANT * q : QUADRANT * q + PACK, :].bitcast(I32),
+                x_scales[0, PACK * q : PACK * (q + 1), :].bitcast(I32),
+            )
         nc.sync.dma_start(w1_raw[0][:], w1_rows[:, :, 0 : H // 2])
         nc.sync.dma_start(w1_raw[1][:], w1_rows[:, :, H // 2 : H])
         nc.sync.dma_start(pos_t[0][:], pos1)
         nc.sync.dma_start(pos_t[1][:], pos2)
 
-        x_code = keep.tile([P, S], U32, name="x_code", align_bytes=64)
-        x_scale = keep.tile([P, S], U8, name="x_scale", align_bytes=64)
+        x_code = keep.tile([P, S], U32, name="x_code", align_bytes=ALIGN)
+        x_scale = keep.tile([P, S], U8, name="x_scale", align_bytes=ALIGN)
         nc.vector.tensor_copy(x_code[:], word_table[:].bitcast(U32).indirect(offs_t[:]))
         nc.vector.tensor_copy(x_scale[:], scale_table[:].indirect(offs_t[:]))
-        pieces = ((0, 256), (256, 384), (384, 512))
 
-        w1_bf = keep.tile([P, PACK * P * PACK], BF16, name="w1_bf", align_bytes=64)
+        w1_bf = keep.tile([P, PACK * P * PACK], BF16, name="w1_bf", align_bytes=ALIGN)
         w1_dst = w1_bf[:].rearrange("p (t m j) -> p m j t", t=PACK, j=PACK)
         w1_src = [w1_raw[c][:].rearrange("p j (m t) -> p m j t", t=PACK) for c in range(2)]
-        nc.scalar.copy(w1_dst[:, 0:64], w1_src[0])
-        nc.vector.tensor_copy(w1_dst[:, 64:P, :, 0:2], w1_src[1][:, :, :, 0:2])
-        nc.scalar.copy(w1_dst[:, 64:P, :, 2:4], w1_src[1][:, :, :, 2:4])
+        nc.scalar.activation(w1_dst[:, 0 : P // 2], w1_src[0], ACT.Copy)
+        nc.vector.tensor_copy(w1_dst[:, P // 2 : P, :, 0:2], w1_src[1][:, :, :, 0:2])
+        nc.scalar.copy(w1_dst[:, P // 2 : P, :, 2:PACK], w1_src[1][:, :, :, 2:PACK])
 
-        w1_code = [keep.tile([P, P], U32, name=f"w1_code{t}", tag=f"code{t}", align_bytes=64) for t in range(PACK)]
-        w1_scale = [keep.tile([P, P], U8, name=f"w1_scale{t}", tag=f"scale{t}", align_bytes=64) for t in range(PACK)]
-
-        def quantize_w1(t):
-            m0, m1 = 0, P
-            nc.vector.quantize_mx(out=w1_code[t][:, m0:m1].bitcast(FP8X4), scales=w1_scale[t][:, m0:m1],
-                                  in_=w1_bf[:, (t * P + m0) * PACK : (t * P + m1) * PACK])
-
+        w1_code = [keep.tile([P, P], U32, name=f"w1_code{t}", tag=f"code{t}", align_bytes=ALIGN) for t in range(PACK)]
+        w1_scale = [keep.tile([P, P], U8, name=f"w1_scale{t}", tag=f"scale{t}", align_bytes=ALIGN) for t in range(PACK)]
         for t in range(PACK):
-            quantize_w1(t)
+            nc.vector.quantize_mx(
+                out=w1_code[t][:].bitcast(FP8X4),
+                scales=w1_scale[t][:],
+                in_=w1_bf[:, t * P * PACK : (t + 1) * P * PACK],
+            )
 
         h = [keep.tile([P, S], F32, name=f"h{t}") for t in range(PACK)]
 
-        def layer1(t, a, b, tag):
-            acc = psum.tile([P, b - a], F32, name="acc", tag=tag)
-            nc.tensor.matmul_mx(out=acc[:], lhsT=w1_code[t][:].bitcast(FP8X4), lhsT_scale=w1_scale[t][:],
-                                rhs=x_code[:, a:b].bitcast(FP8X4), rhs_scale=x_scale[:, a:b], start=True, stop=True)
-            if t == 0 and a == 256:
-                nc.vector.tensor_scalar(h[t][:, a:b], acc[:], 0.0, None, ALU.max)
+        def layer1(t, first, end, bank, on_vector):
+            acc = psum.tile([P, end - first], F32, name="acc", tag=f"bank{bank}")
+            nc.tensor.matmul_mx(
+                out=acc[:],
+                lhsT=w1_code[t][:].bitcast(FP8X4),
+                lhsT_scale=w1_scale[t][:],
+                rhs=x_code[:, first:end].bitcast(FP8X4),
+                rhs_scale=x_scale[:, first:end],
+                start=True,
+                stop=True,
+            )
+            if on_vector:
+                nc.vector.tensor_scalar(h[t][:, first:end], acc[:], 0.0, None, ALU.max)
             else:
-                nc.scalar.activation(h[t][:, a:b], acc[:], ACT.Relu)
+                nc.scalar.activation(h[t][:, first:end], acc[:], ACT.Relu)
 
-        for i, (a, b) in enumerate(pieces):
-            layer1(0, a, b, f"bank{i}")
+        for piece, (first, end) in enumerate(PLANE0_PIECES):
+            layer1(0, first, end, piece, piece == PLANE0_PIECE_ON_VECTOR)
         for t in range(1, PACK):
-            layer1(t, 0, S, f"bank{2 + t}")
+            layer1(t, 0, S, len(PLANE0_PIECES) + t - 1, False)
 
         w23_raw = keep.tile([P, 2 * PACK * N], F32, name="w23_raw")
         w2_raw = w23_raw[:, 0 : PACK * N]
         w3_raw = w23_raw[:, PACK * N :]
         nc.sync.dma_start(w2_raw, w2.rearrange("(p j) n -> p (j n)", j=PACK))
         nc.sync.dma_start(w3_raw, w3.rearrange("(p j) n -> p (j n)", j=PACK))
-        w23_bf = keep.tile([P, 2 * N * PACK], BF16, name="w23_bf", tag="scale3", align_bytes=64)
-        w23_dst = w23_bf[:].rearrange("p (w c i j) -> p w c j i", w=2, i=4, j=PACK)
-        nc.scalar.copy(w23_dst[:, 0], w2_raw.rearrange("p (j c i) -> p c j i", j=PACK, i=4))
-        nc.scalar.activation(w23_dst[:, 1], w3_raw.rearrange("p (j c i) -> p c j i", j=PACK, i=4), ACT.Copy, scale=half[:])
-        w23_code = keep.tile([P, 2 * N], U32, name="w23_code", align_bytes=64)
-        w23_scale = keep.tile([P, 2 * N], U8, name="w23_scale", align_bytes=64)
+        w23_bf = keep.tile([P, 2 * N * PACK], BF16, name="w23_bf", tag=f"scale{PACK - 1}", align_bytes=ALIGN)
+        w23_dst = w23_bf[:].rearrange("p (w c i j) -> p w c j i", w=2, i=RUN, j=PACK)
+        nc.scalar.copy(w23_dst[:, 0], w2_raw.rearrange("p (j c i) -> p c j i", j=PACK, i=RUN))
+        nc.scalar.copy(w23_dst[:, 1], w3_raw.rearrange("p (j c i) -> p c j i", j=PACK, i=RUN))
+        w23_code = keep.tile([P, 2 * N], U32, name="w23_code", align_bytes=ALIGN)
+        w23_scale = keep.tile([P, 2 * N], U8, name="w23_scale", align_bytes=ALIGN)
 
         nbr = [keep.tile([P, PACK, V], F32, name=f"nbr{d}", tag=f"nbr{d}") for d in range(2)]
-        sum_t = keep.tile([P, 2 * HALF * PACK], BF16, name="sum_t", tag="code3", align_bytes=64)
-        back = [psum.tile([P, 2, HALF], F32, name="back", tag=f"bank{4 + u}") for u in range(2)]
+        z_turned = keep.tile([P, 2 * HALF * PACK], BF16, name="z_turned", tag=f"code{PACK - 1}", align_bytes=ALIGN)
+        z_words = [psum.tile([P, 2, HALF], F32, name="z_words", tag=f"bank{4 + u}") for u in range(2)]
         for pair in range(2):
             turned = [psum.tile([P, 2, P], F32, name="turned", tag=f"bank{2 * pair + u}") for u in range(2)]
             for e in range(2):
@@ -119,46 +130,80 @@ def tile_picked_sagecat_mean_p_kernel(tc, x_words, x_scales, w1, w2, w3, offs, c
                 for d in range(2):
                     nc.vector.tensor_copy(nbr[d][:, t, :], h[t][:].indirect(pos_t[d][:]))
                     for u in range(2):
-                        nc.tensor.matmul(turned[u][:, e, :], nbr[d][:, t, u * HALF : (u + 1) * HALF], ident[:],
-                                         is_transpose=True, start=(d == 0), stop=(d == 1))
+                        nc.tensor.matmul(
+                            turned[u][:, e, :],
+                            nbr[d][:, t, u * HALF : (u + 1) * HALF],
+                            ident[:],
+                            is_transpose=True,
+                            start=(d == 0),
+                            stop=(d == 1),
+                        )
+            rounded = [z_turned[:, (2 * u + pair) * 2 * P : (2 * u + pair + 1) * 2 * P] for u in range(2)]
             for u in range(2):
-                lo = (2 * u + pair) * 2 * P
-                nc.scalar.copy(sum_t[:, lo : lo + 2 * P].rearrange("p (m e) -> p m e", e=2), turned[u][:].rearrange("p e m -> p m e"))
+                nc.scalar.activation(
+                    rounded[u].rearrange("p (m e) -> p m e", e=2),
+                    turned[u][:].rearrange("p e m -> p m e"),
+                    ACT.Copy,
+                    scale=0.5,
+                )
             for u in range(2):
-                lo = (2 * u + pair) * 2 * P
-                nc.tensor.transpose(back[u][:, pair, :], sum_t[:, lo : lo + 2 * P].bitcast(F32), ident[:])
+                nc.tensor.transpose(z_words[u][:, pair, :], rounded[u].bitcast(F32), ident[:])
             if pair == 0:
                 nc.vector.quantize_mx(out=w23_code[:].bitcast(FP8X4), scales=w23_scale[:], in_=w23_bf[:])
 
-        sum_bf = keep.tile([P, V * PACK], BF16, name="sum_bf", align_bytes=64)
+        z_bf = keep.tile([P, V * PACK], BF16, name="z_bf", align_bytes=ALIGN)
         for u in range(2):
-            nc.scalar.copy(sum_bf[:, u * HALF * PACK : (u + 1) * HALF * PACK].bitcast(F32).rearrange("p (v w) -> p v w", w=2),
-                           back[u][:].rearrange("p w v -> p v w"))
+            nc.scalar.copy(
+                z_bf[:, u * HALF * PACK : (u + 1) * HALF * PACK].bitcast(F32).rearrange("p (v w) -> p v w", w=2),
+                z_words[u][:].rearrange("p w v -> p v w"),
+            )
 
-        split = 192
-        own = keep.tile([P, PACK, split], F32, name="own", tag="nbr0")
-        own_bf = keep.tile([P, V * PACK], BF16, name="own_bf", tag="code3", align_bytes=64)
+        own = keep.tile([P, PACK, OWN_SPLIT], F32, name="own", tag="nbr0")
+        own_bf = keep.tile([P, V * PACK], BF16, name="own_bf", tag=f"code{PACK - 1}", align_bytes=ALIGN)
         for t in range(PACK):
-            nc.vector.tensor_copy(own[:, t, :], h[t][:].indirect(cen_t[:, 0 : split // LIST]))
-        for a, b in ((0, HALF), (HALF, split)):
-            nc.scalar.copy(own_bf[:, a * PACK : b * PACK].rearrange("p (c i t) -> p c t i", i=4, t=PACK),
-                           own[:, :, a:b].rearrange("p t (c i) -> p c t i", i=4))
+            nc.vector.tensor_copy(own[:, t, :], h[t][:].indirect(cen_t[:, 0 : OWN_SPLIT // LIST]))
+        for first, end in ((0, HALF), (HALF, OWN_SPLIT)):
+            nc.scalar.copy(
+                own_bf[:, first * PACK : end * PACK].rearrange("p (c i t) -> p c t i", i=RUN, t=PACK),
+                own[:, :, first:end].rearrange("p t (c i) -> p c t i", i=RUN),
+            )
         for t in range(PACK):
-            nc.vector.tensor_copy(own_bf[:, split * PACK + t : V * PACK : PACK], h[t][:].indirect(cen_t[:, split // LIST :]))
+            nc.vector.tensor_copy(
+                own_bf[:, OWN_SPLIT * PACK + t : V * PACK : PACK],
+                h[t][:].indirect(cen_t[:, OWN_SPLIT // LIST :]),
+            )
 
-        sum_code = keep.tile([P, V], U32, name="sum_code", align_bytes=64)
-        sum_scale = keep.tile([P, V], U8, name="sum_scale", align_bytes=64)
-        nc.vector.quantize_mx(out=sum_code[:].bitcast(FP8X4), scales=sum_scale[:], in_=sum_bf[:])
+        z_code = keep.tile([P, V], U32, name="z_code", align_bytes=ALIGN)
+        z_scale = keep.tile([P, V], U8, name="z_scale", align_bytes=ALIGN)
+        nc.vector.quantize_mx(out=z_code[:].bitcast(FP8X4), scales=z_scale[:], in_=z_bf[:])
         for u in range(2):
             cols = slice(u * HALF, (u + 1) * HALF)
-            own_code = keep.tile([P, HALF], U32, name=f"own_code{u}", align_bytes=64)
-            own_scale = keep.tile([P, HALF], U8, name=f"own_scale{u}", align_bytes=64)
-            nc.vector.quantize_mx(out=own_code[:].bitcast(FP8X4), scales=own_scale[:], in_=own_bf[:, u * HALF * PACK : (u + 1) * HALF * PACK])
-            acc = psum.tile([P, HALF], F32, name=f"acc_out{u}")
-            nc.tensor.matmul_mx(out=acc[:], lhsT=w23_code[:, N : 2 * N].bitcast(FP8X4), lhsT_scale=w23_scale[:, N : 2 * N],
-                                rhs=sum_code[:, cols].bitcast(FP8X4), rhs_scale=sum_scale[:, cols], start=True, stop=False)
-            nc.tensor.matmul_mx(out=acc[:], lhsT=w23_code[:, 0:N].bitcast(FP8X4), lhsT_scale=w23_scale[:, 0:N],
-                                rhs=own_code[:].bitcast(FP8X4), rhs_scale=own_scale[:], start=False, stop=True)
+            own_code = keep.tile([P, HALF], U32, name=f"own_code{u}", align_bytes=ALIGN)
+            own_scale = keep.tile([P, HALF], U8, name=f"own_scale{u}", align_bytes=ALIGN)
+            nc.vector.quantize_mx(
+                out=own_code[:].bitcast(FP8X4),
+                scales=own_scale[:],
+                in_=own_bf[:, u * HALF * PACK : (u + 1) * HALF * PACK],
+            )
+            acc_out = psum.tile([P, HALF], F32, name=f"acc_out{u}")
+            nc.tensor.matmul_mx(
+                out=acc_out[:],
+                lhsT=w23_code[:, N : 2 * N].bitcast(FP8X4),
+                lhsT_scale=w23_scale[:, N : 2 * N],
+                rhs=z_code[:, cols].bitcast(FP8X4),
+                rhs_scale=z_scale[:, cols],
+                start=True,
+                stop=False,
+            )
+            nc.tensor.matmul_mx(
+                out=acc_out[:],
+                lhsT=w23_code[:, 0:N].bitcast(FP8X4),
+                lhsT_scale=w23_scale[:, 0:N],
+                rhs=own_code[:].bitcast(FP8X4),
+                rhs_scale=own_scale[:],
+                start=False,
+                stop=True,
+            )
             res = keep.tile([P, HALF], F32, name=f"res{u}")
-            nc.scalar.copy(res[:], acc[:])
+            nc.scalar.copy(res[:], acc_out[:])
             nc.sync.dma_start(out[:, cols], res[:])

@@ -49,8 +49,7 @@ def tile_picked_sagecat_mean_p_kernel(tc, x_words, x_scales, w1, w2, w3, offs, c
         nc.vector.memset(ident[:], 0.0)
         make_identity(nc, ident[:], nomemset=True)
 
-        w1_rows = w1.rearrange("(p j) c -> p j c", j=PACK)
-        w1_raw = [keep.tile([P, PACK, H // 2], F32, name=f"w1_raw{c}") for c in range(2)]
+        w1_raw = keep.tile([P, PACK * H], F32, name="w1_raw")
         nc.sync.dma_start(offs_t[:], offs)
         nc.sync.dma_start(word_table[:], x_words[0].rearrange("p n t -> p (n t)").bitcast(I32))
         nc.sync.dma_start(cen_t[:], cen)
@@ -59,8 +58,7 @@ def tile_picked_sagecat_mean_p_kernel(tc, x_words, x_scales, w1, w2, w3, offs, c
                 scale_table[QUADRANT * q : QUADRANT * q + PACK, :].bitcast(I32),
                 x_scales[0, PACK * q : PACK * (q + 1), :].bitcast(I32),
             )
-        nc.sync.dma_start(w1_raw[0][:], w1_rows[:, :, 0 : H // 2])
-        nc.sync.dma_start(w1_raw[1][:], w1_rows[:, :, H // 2 : H])
+        nc.sync.dma_start(w1_raw[:], w1.rearrange("(p j) c -> p (j c)", j=PACK))
         nc.sync.dma_start(pos_t[0][:], pos1)
         nc.sync.dma_start(pos_t[1][:], pos2)
 
@@ -69,21 +67,21 @@ def tile_picked_sagecat_mean_p_kernel(tc, x_words, x_scales, w1, w2, w3, offs, c
         nc.vector.tensor_copy(x_code[:], word_table[:].bitcast(U32).indirect(offs_t[:]))
         nc.vector.tensor_copy(x_scale[:], scale_table[:].indirect(offs_t[:]))
 
-        w1_bf = keep.tile([P, PACK * P * PACK], BF16, name="w1_bf", align_bytes=ALIGN)
-        w1_dst = w1_bf[:].rearrange("p (t m j) -> p m j t", t=PACK, j=PACK)
-        w1_src = [w1_raw[c][:].rearrange("p j (m t) -> p m j t", t=PACK) for c in range(2)]
-        nc.scalar.activation(w1_dst[:, 0 : P // 2], w1_src[0], ACT.Copy)
-        nc.vector.tensor_copy(w1_dst[:, P // 2 : P, :, 0:2], w1_src[1][:, :, :, 0:2])
-        nc.scalar.copy(w1_dst[:, P // 2 : P, :, 2:PACK], w1_src[1][:, :, :, 2:PACK])
-
+        w1_bf = [keep.tile([P, P * PACK], BF16, name=f"w1_bf{t}", tag=("w1_bf0", "w1_bf1", "w1_bf0", "w1_bf3")[t], align_bytes=ALIGN) for t in range(PACK)]
+        w1_src = w1_raw[:].rearrange("p (j b t r i) -> p t b r j i", j=PACK, t=PACK, r=2, i=RUN)
         w1_code = [keep.tile([P, P], U32, name=f"w1_code{t}", tag=f"code{t}", align_bytes=ALIGN) for t in range(PACK)]
         w1_scale = [keep.tile([P, P], U8, name=f"w1_scale{t}", tag=f"scale{t}", align_bytes=ALIGN) for t in range(PACK)]
         for t in range(PACK):
-            nc.vector.quantize_mx(
-                out=w1_code[t][:].bitcast(FP8X4),
-                scales=w1_scale[t][:],
-                in_=w1_bf[:, t * P * PACK : (t + 1) * P * PACK],
-            )
+            w1_dst = w1_bf[t][:].rearrange("p (b r i j) -> p b r j i", r=2, i=RUN, j=PACK)
+            if t == 0:
+                for r in range(2):
+                    nc.scalar.activation(w1_dst[:, 0:8, r], w1_src[:, t, 0:8, r], ACT.Copy)
+                nc.vector.tensor_copy(w1_dst[:, 8:16], w1_src[:, t, 8:16])
+            elif t != 2:
+                nc.scalar.copy(w1_dst, w1_src[:, t])
+            else:
+                nc.vector.tensor_copy(w1_dst, w1_src[:, t])
+            nc.vector.quantize_mx(out=w1_code[t][:].bitcast(FP8X4), scales=w1_scale[t][:], in_=w1_bf[t][:])
 
         h = [keep.tile([P, S], F32, name=f"h{t}") for t in range(PACK)]
 
@@ -111,8 +109,9 @@ def tile_picked_sagecat_mean_p_kernel(tc, x_words, x_scales, w1, w2, w3, offs, c
         w23_raw = keep.tile([P, 2 * PACK * N], F32, name="w23_raw")
         w2_raw = w23_raw[:, 0 : PACK * N]
         w3_raw = w23_raw[:, PACK * N :]
-        nc.sync.dma_start(w2_raw, w2.rearrange("(p j) n -> p (j n)", j=PACK))
-        nc.sync.dma_start(w3_raw, w3.rearrange("(p j) n -> p (j n)", j=PACK))
+        for raw, w in ((w2_raw, w2), (w3_raw, w3)):
+            for t in range(PACK):
+                nc.sync.dma_start(raw[:, t * N : (t + 1) * N], w.rearrange("(b t r) n -> t b r n", t=PACK, r=8)[t])
         w23_bf = keep.tile([P, 2 * N * PACK], BF16, name="w23_bf", tag=f"scale{PACK - 1}", align_bytes=ALIGN)
         w23_dst = w23_bf[:].rearrange("p (w c i j) -> p w c j i", w=2, i=RUN, j=PACK)
         nc.scalar.copy(w23_dst[:, 0], w2_raw.rearrange("p (j c i) -> p c j i", j=PACK, i=RUN))

@@ -50,8 +50,8 @@ def tile_picked_sagecat_mean_p_kernel(tc, x_words, x_scales, w1, w2, w3, offs, c
         make_identity(nc, ident[:], nomemset=True)
 
         w1_raw = keep.tile([P, PACK * H], F32, name="w1_raw")
-        nc.sync.dma_start(offs_t[:], offs)
         nc.sync.dma_start(word_table[:], x_words[0].rearrange("p n t -> p (n t)").bitcast(I32))
+        nc.sync.dma_start(offs_t[:], offs)
         nc.sync.dma_start(cen_t[:], cen)
         for q in range(P // QUADRANT):
             nc.sync.dma_start(

@@ -1,7 +1,6 @@
 from contextlib import ExitStack
 
 import concourse.mybir as mybir
-from concourse.masks import make_identity
 
 K, T, S, V, H, N = 512, 1024, 512, 256, 512, 128
 FLOPS = 2 * K * S * H + 2 * 2 * H * V * N
@@ -27,8 +26,6 @@ ALIGN = 64
 PLANE0_PIECES = ((0, 256), (256, 384), (384, S))
 PLANE0_PIECE_ON_VECTOR = 1
 
-OWN_SPLIT = 192
-
 
 def tile_picked_sagecat_mean_p_kernel(tc, x_words, x_scales, w1, w2, w3, offs, cen, pos1, pos2, out):
     nc = tc.nc
@@ -44,10 +41,6 @@ def tile_picked_sagecat_mean_p_kernel(tc, x_words, x_scales, w1, w2, w3, offs, c
         scale_table = keep.tile([P, T], U8, name="scale_table", align_bytes=ALIGN)
         word_table = keep.tile([P, T], I32, name="word_table", align_bytes=ALIGN)
         nc.vector.memset(scale_table[:].bitcast(I32), 0)
-
-        ident = keep.tile([P, P], F32, name="ident")
-        nc.vector.memset(ident[:], 0.0)
-        make_identity(nc, ident[:], nomemset=True)
 
         w1_raw = keep.tile([P, PACK * H], F32, name="w1_raw")
         nc.sync.dma_start(word_table[:], x_words[0].rearrange("p n t -> p (n t)").bitcast(I32))
@@ -116,93 +109,63 @@ def tile_picked_sagecat_mean_p_kernel(tc, x_words, x_scales, w1, w2, w3, offs, c
         w23_dst = w23_bf[:].rearrange("p (w c i j) -> p w c j i", w=2, i=RUN, j=PACK)
         nc.scalar.copy(w23_dst[:, 0], w2_raw.rearrange("p (j c i) -> p c j i", j=PACK, i=RUN))
         nc.scalar.copy(w23_dst[:, 1], w3_raw.rearrange("p (j c i) -> p c j i", j=PACK, i=RUN))
-        w23_code = keep.tile([P, 2 * N], U32, name="w23_code", align_bytes=ALIGN)
         w23_scale = keep.tile([P, 2 * N], U8, name="w23_scale", align_bytes=ALIGN)
 
-        nbr = [keep.tile([P, PACK, V], F32, name=f"nbr{d}", tag=f"nbr{d}") for d in range(2)]
-        z_turned = keep.tile([P, 2 * HALF * PACK], BF16, name="z_turned", tag=f"code{PACK - 1}", align_bytes=ALIGN)
-        z_words = [psum.tile([P, 2, HALF], F32, name="z_words", tag=f"bank{4 + u}") for u in range(2)]
-        for pair in range(2):
-            turned = [psum.tile([P, 2, P], F32, name="turned", tag=f"bank{2 * pair + u}") for u in range(2)]
-            for e in range(2):
-                t = 2 * pair + e
-                for d in range(2):
-                    nc.vector.tensor_copy(nbr[d][:, t, :], h[t][:].indirect(pos_t[d][:]))
-                    for u in range(2):
-                        nc.tensor.matmul(
-                            turned[u][:, e, :],
-                            nbr[d][:, t, u * HALF : (u + 1) * HALF],
-                            ident[:],
-                            is_transpose=True,
-                            start=(d == 0),
-                            stop=(d == 1),
-                        )
-            rounded = [z_turned[:, (2 * u + pair) * 2 * P : (2 * u + pair + 1) * 2 * P] for u in range(2)]
-            for u in range(2):
-                nc.scalar.activation(
-                    rounded[u].rearrange("p (m e) -> p m e", e=2),
-                    turned[u][:].rearrange("p e m -> p m e"),
-                    ACT.Copy,
-                    scale=0.5,
-                )
-            for u in range(2):
-                nc.tensor.transpose(z_words[u][:, pair, :], rounded[u].bitcast(F32), ident[:])
-            if pair == 0:
+        z_sum = [keep.tile([P, 2, V], F32, name=f"z_sum{pair}") for pair in range(2)]
+        own = [keep.tile([P, 2, (V, HALF)[pair]], F32, name=f"own{pair}") for pair in range(2)]
+        z_bf = [keep.tile([P, HALF * PACK], BF16, name=f"z_bf{u}", align_bytes=ALIGN) for u in range(2)]
+        own_bf = [keep.tile([P, HALF * PACK], BF16, name="own_bf0", align_bytes=ALIGN)]
+
+        def pair_slots(tile, pair):
+            return tile[:].rearrange("p (v g e) -> p g v e", g=2, e=2)[:, pair]
+
+        def pair_values(tile, u):
+            return tile[:, :, u * HALF : (u + 1) * HALF].rearrange("p e v -> p v e")
+
+        for t in range(PACK):
+            pair, e = divmod(t, 2)
+            nbr = keep.tile([P, V], F32, name=f"nbr{t}", tag=f"nbr{t}", align_bytes=ALIGN)
+            nc.vector.tensor_copy(nbr[:], h[t][:].indirect(pos_t[0][:]))
+            if t == PACK - 1:
+                w23_code = keep.tile([P, 2 * N], U32, name="w23_code", tag="nbr1", align_bytes=ALIGN)
                 nc.vector.quantize_mx(out=w23_code[:].bitcast(FP8X4), scales=w23_scale[:], in_=w23_bf[:])
+            width = (V, HALF)[pair]
+            nc.vector.tensor_copy(own[pair][:, e, :], h[t][:].indirect(cen_t[:, 0 : width // LIST]))
+            nc.vector.tensor_tensor(z_sum[pair][:, e, :], h[t][:].indirect(pos_t[1][:]), nbr[:], ALU.add)
+            if e == 1:
+                nc.scalar.copy(pair_slots(own_bf[0], pair), pair_values(own[pair], 0))
+                for u in range(2):
+                    nc.scalar.activation(pair_slots(z_bf[u], pair), pair_values(z_sum[pair], u), ACT.Copy, scale=0.5)
+            if t == 2:
+                own_bf.append(keep.tile([P, HALF * PACK], BF16, name="own_bf1", tag="nbr2", align_bytes=ALIGN))
+                nc.scalar.copy(pair_slots(own_bf[1], 0), pair_values(own[0], 1))
+        for t in range(2, PACK):
+            nc.vector.tensor_copy(own_bf[1][:, t : HALF * PACK : PACK], h[t][:].indirect(cen_t[:, HALF // LIST :]))
 
-        z_bf = keep.tile([P, V * PACK], BF16, name="z_bf", align_bytes=ALIGN)
-        for u in range(2):
-            nc.scalar.copy(
-                z_bf[:, u * HALF * PACK : (u + 1) * HALF * PACK].bitcast(F32).rearrange("p (v w) -> p v w", w=2),
-                z_words[u][:].rearrange("p w v -> p v w"),
-            )
+        acc_out = [psum.tile([P, HALF], F32, name=f"acc_out{u}") for u in range(2)]
 
-        own = keep.tile([P, PACK, OWN_SPLIT], F32, name="own", tag="nbr0")
-        own_bf = keep.tile([P, V * PACK], BF16, name="own_bf", tag=f"code{PACK - 1}", align_bytes=ALIGN)
-        for t in range(PACK):
-            nc.vector.tensor_copy(own[:, t, :], h[t][:].indirect(cen_t[:, 0 : OWN_SPLIT // LIST]))
-        for first, end in ((0, HALF), (HALF, OWN_SPLIT)):
-            nc.scalar.copy(
-                own_bf[:, first * PACK : end * PACK].rearrange("p (c i t) -> p c t i", i=RUN, t=PACK),
-                own[:, :, first:end].rearrange("p t (c i) -> p c t i", i=RUN),
-            )
-        for t in range(PACK):
-            nc.vector.tensor_copy(
-                own_bf[:, OWN_SPLIT * PACK + t : V * PACK : PACK],
-                h[t][:].indirect(cen_t[:, OWN_SPLIT // LIST :]),
-            )
-
-        z_code = keep.tile([P, V], U32, name="z_code", align_bytes=ALIGN)
-        z_scale = keep.tile([P, V], U8, name="z_scale", align_bytes=ALIGN)
-        nc.vector.quantize_mx(out=z_code[:].bitcast(FP8X4), scales=z_scale[:], in_=z_bf[:])
-        for u in range(2):
-            cols = slice(u * HALF, (u + 1) * HALF)
-            own_code = keep.tile([P, HALF], U32, name=f"own_code{u}", align_bytes=ALIGN)
-            own_scale = keep.tile([P, HALF], U8, name=f"own_scale{u}", align_bytes=ALIGN)
-            nc.vector.quantize_mx(
-                out=own_code[:].bitcast(FP8X4),
-                scales=own_scale[:],
-                in_=own_bf[:, u * HALF * PACK : (u + 1) * HALF * PACK],
-            )
-            acc_out = psum.tile([P, HALF], F32, name=f"acc_out{u}")
+        def layer2(u, w, values, name, first):
+            code = keep.tile([P, HALF], U32, name=f"{name}_code{u}", align_bytes=ALIGN)
+            scale = keep.tile([P, HALF], U8, name=f"{name}_scale{u}", align_bytes=ALIGN)
+            nc.vector.quantize_mx(out=code[:].bitcast(FP8X4), scales=scale[:], in_=values[:])
             nc.tensor.matmul_mx(
-                out=acc_out[:],
-                lhsT=w23_code[:, N : 2 * N].bitcast(FP8X4),
-                lhsT_scale=w23_scale[:, N : 2 * N],
-                rhs=z_code[:, cols].bitcast(FP8X4),
-                rhs_scale=z_scale[:, cols],
-                start=True,
-                stop=False,
+                out=acc_out[u][:],
+                lhsT=w23_code[:, w * N : (w + 1) * N].bitcast(FP8X4),
+                lhsT_scale=w23_scale[:, w * N : (w + 1) * N],
+                rhs=code[:].bitcast(FP8X4),
+                rhs_scale=scale[:],
+                start=first,
+                stop=not first,
             )
-            nc.tensor.matmul_mx(
-                out=acc_out[:],
-                lhsT=w23_code[:, 0:N].bitcast(FP8X4),
-                lhsT_scale=w23_scale[:, 0:N],
-                rhs=own_code[:].bitcast(FP8X4),
-                rhs_scale=own_scale[:],
-                start=False,
-                stop=True,
-            )
+
+        def store(u):
             res = keep.tile([P, HALF], F32, name=f"res{u}")
-            nc.scalar.copy(res[:], acc_out[:])
-            nc.sync.dma_start(out[:, cols], res[:])
+            nc.scalar.copy(res[:], acc_out[u][:])
+            nc.sync.dma_start(out[:, u * HALF : (u + 1) * HALF], res[:])
+
+        layer2(0, 0, own_bf[0], "own", True)
+        layer2(0, 1, z_bf[0], "z", False)
+        store(0)
+        layer2(1, 0, own_bf[1], "own", True)
+        layer2(1, 1, z_bf[1], "z", False)
+        store(1)

@@ -26,12 +26,15 @@ ALIGN = 64
 PLANE0_PIECES = ((0, 256), (256, 384), (384, S))
 PLANE0_PIECE_ON_VECTOR = 1
 
+LAST_PIECES = ((0, 128), (128, 192), (192, V))
+
 
 def tile_picked_sagecat_mean_p_kernel(tc, x_words, x_scales, w1, w2, w3, offs, cen, pos1, pos2, out):
     nc = tc.nc
     with ExitStack() as ctx:
         lists = ctx.enter_context(tc.tile_pool(name="lists", bufs=1))
         keep = ctx.enter_context(tc.tile_pool(name="keep", bufs=1))
+        shared = ctx.enter_context(tc.tile_pool(name="shared", bufs=1))
         psum = ctx.enter_context(tc.psum_pool(name="psum", bufs=1))
 
         offs_t = lists.tile([P, S // LIST], U16, name="offs_t")
@@ -99,9 +102,10 @@ def tile_picked_sagecat_mean_p_kernel(tc, x_words, x_scales, w1, w2, w3, offs, c
         for t in range(1, PACK):
             layer1(t, 0, S, len(PLANE0_PIECES) + t - 1, False)
 
-        w23_raw = keep.tile([P, 2 * PACK * N], F32, name="w23_raw")
-        w2_raw = w23_raw[:, 0 : PACK * N]
-        w3_raw = w23_raw[:, PACK * N :]
+        w2_tile = shared.tile([P, PACK * N], F32, name="w2_tile", offset=0, align_bytes=ALIGN)
+        w3_tile = keep.tile([P, PACK * N], F32, name="w3_tile")
+        w2_raw = w2_tile[:]
+        w3_raw = w3_tile[:]
         for raw, w in ((w2_raw, w2), (w3_raw, w3)):
             for t in range(PACK):
                 nc.sync.dma_start(raw[:, t * N : (t + 1) * N], w.rearrange("(b t r) n -> t b r n", t=PACK, r=8)[t])
@@ -109,63 +113,74 @@ def tile_picked_sagecat_mean_p_kernel(tc, x_words, x_scales, w1, w2, w3, offs, c
         w23_dst = w23_bf[:].rearrange("p (w c i j) -> p w c j i", w=2, i=RUN, j=PACK)
         nc.scalar.copy(w23_dst[:, 0], w2_raw.rearrange("p (j c i) -> p c j i", j=PACK, i=RUN))
         nc.scalar.copy(w23_dst[:, 1], w3_raw.rearrange("p (j c i) -> p c j i", j=PACK, i=RUN))
-        w23_scale = keep.tile([P, 2 * N], U8, name="w23_scale", align_bytes=ALIGN)
 
-        z_sum = [keep.tile([P, 2, V], F32, name=f"z_sum{pair}") for pair in range(2)]
-        own = [keep.tile([P, 2, (V, HALF)[pair]], F32, name=f"own{pair}") for pair in range(2)]
+        own = [keep.tile([P, 2, V], F32, name=f"own{pair}") for pair in range(2)]
+        own_bf = keep.tile([P, V * PACK], BF16, name="own_bf", align_bytes=ALIGN)
         z_bf = [keep.tile([P, HALF * PACK], BF16, name=f"z_bf{u}", align_bytes=ALIGN) for u in range(2)]
-        own_bf = [keep.tile([P, HALF * PACK], BF16, name="own_bf0", align_bytes=ALIGN)]
+        held_at = PACK * N * 4
+        nbr = [keep.tile([P, V], F32, name=f"nbr{t}") for t in (0, 1, 3)]
+        nbr.insert(2, shared.tile([P, V], F32, name="nbr2", offset=held_at, align_bytes=ALIGN))
 
-        def pair_slots(tile, pair):
-            return tile[:].rearrange("p (v g e) -> p g v e", g=2, e=2)[:, pair]
+        def pair_slots(values, pair):
+            return values.rearrange("p (v g e) -> p g v e", g=2, e=2)[:, pair]
 
-        def pair_values(tile, u):
-            return tile[:, :, u * HALF : (u + 1) * HALF].rearrange("p e v -> p v e")
+        def gather_first(t):
+            nc.vector.tensor_copy(nbr[t][:], h[t][:].indirect(pos_t[0][:]))
+            nc.vector.tensor_copy(own[t // 2][:, t % 2, :], h[t][:].indirect(cen_t[:]))
 
-        for t in range(PACK):
-            pair, e = divmod(t, 2)
-            nbr = keep.tile([P, V], F32, name=f"nbr{t}", tag=f"nbr{t}", align_bytes=ALIGN)
-            nc.vector.tensor_copy(nbr[:], h[t][:].indirect(pos_t[0][:]))
-            if t == PACK - 1:
-                w23_code = keep.tile([P, 2 * N], U32, name="w23_code", tag="nbr1", align_bytes=ALIGN)
-                nc.vector.quantize_mx(out=w23_code[:].bitcast(FP8X4), scales=w23_scale[:], in_=w23_bf[:])
-            width = (V, HALF)[pair]
-            nc.vector.tensor_copy(own[pair][:, e, :], h[t][:].indirect(cen_t[:, 0 : width // LIST]))
-            nc.vector.tensor_tensor(z_sum[pair][:, e, :], h[t][:].indirect(pos_t[1][:]), nbr[:], ALU.add)
-            if e == 1:
-                nc.scalar.copy(pair_slots(own_bf[0], pair), pair_values(own[pair], 0))
-                for u in range(2):
-                    nc.scalar.activation(pair_slots(z_bf[u], pair), pair_values(z_sum[pair], u), ACT.Copy, scale=0.5)
-            if t == 2:
-                own_bf.append(keep.tile([P, HALF * PACK], BF16, name="own_bf1", tag="nbr2", align_bytes=ALIGN))
-                nc.scalar.copy(pair_slots(own_bf[1], 0), pair_values(own[0], 1))
+        def gather_add(t, first, end, total):
+            places = pos_t[1][:, first // LIST : end // LIST]
+            nc.vector.tensor_tensor(total, h[t][:].indirect(places), nbr[t][:, first:end], ALU.add)
+
+        def round_own(pair):
+            nc.scalar.copy(pair_slots(own_bf[:], pair), own[pair][:].rearrange("p e v -> p v e"))
+
+        def round_mean(pair, first, end, total):
+            u, at = divmod(first, HALF)
+            slots = pair_slots(z_bf[u][:, at * PACK : (at + end - first) * PACK], pair)
+            nc.scalar.activation(slots, total.rearrange("p e v -> p v e"), ACT.Copy, scale=0.5)
+
+        z_sum = keep.tile([P, 2, V], F32, name="z_sum")
+        for t in range(2):
+            gather_first(t)
+            gather_add(t, 0, V, z_sum[:, t, :])
+        round_own(0)
+        for u in range(2):
+            round_mean(0, u * HALF, (u + 1) * HALF, z_sum[:, :, u * HALF : (u + 1) * HALF])
         for t in range(2, PACK):
-            nc.vector.tensor_copy(own_bf[1][:, t : HALF * PACK : PACK], h[t][:].indirect(cen_t[:, HALF // LIST :]))
+            gather_first(t)
+        round_own(1)
+        for first, end in LAST_PIECES:
+            piece = shared.tile([P, 2, end - first], F32, name=f"piece{first}", offset=first * 8, align_bytes=ALIGN)
+            for e in range(2):
+                gather_add(2 + e, first, end, piece[:, e, :])
+            round_mean(1, first, end, piece[:])
+
+        def quantize(name, values, slot):
+            code = keep.tile([P, HALF], U32, name=f"{name}_code", align_bytes=ALIGN)
+            scale = shared.tile([P, HALF], U8, name=f"{name}_scale", offset=held_at + slot * HALF, align_bytes=ALIGN)
+            nc.vector.quantize_mx(out=code[:].bitcast(FP8X4), scales=scale[:], in_=values)
+            return code, scale
 
         acc_out = [psum.tile([P, HALF], F32, name=f"acc_out{u}") for u in range(2)]
 
-        def layer2(u, w, values, name, first):
-            code = keep.tile([P, HALF], U32, name=f"{name}_code{u}", align_bytes=ALIGN)
-            scale = keep.tile([P, HALF], U8, name=f"{name}_scale{u}", align_bytes=ALIGN)
-            nc.vector.quantize_mx(out=code[:].bitcast(FP8X4), scales=scale[:], in_=values[:])
+        def layer2(u, weights, values, first):
             nc.tensor.matmul_mx(
                 out=acc_out[u][:],
-                lhsT=w23_code[:, w * N : (w + 1) * N].bitcast(FP8X4),
-                lhsT_scale=w23_scale[:, w * N : (w + 1) * N],
-                rhs=code[:].bitcast(FP8X4),
-                rhs_scale=scale[:],
+                lhsT=weights[0][:].bitcast(FP8X4),
+                lhsT_scale=weights[1][:],
+                rhs=values[0][:].bitcast(FP8X4),
+                rhs_scale=values[1][:],
                 start=first,
                 stop=not first,
             )
 
-        def store(u):
+        w2_mx = quantize("w2", w23_bf[:, 0 : N * PACK], 0)
+        for u in range(2):
+            layer2(u, w2_mx, quantize(f"own{u}", own_bf[:, u * HALF * PACK : (u + 1) * HALF * PACK], 1 + u), True)
+        w3_mx = quantize("w3", w23_bf[:, N * PACK :], 3)
+        for u in range(2):
+            layer2(u, w3_mx, quantize(f"z{u}", z_bf[u][:], 4 + u), False)
             res = keep.tile([P, HALF], F32, name=f"res{u}")
             nc.scalar.copy(res[:], acc_out[u][:])
             nc.sync.dma_start(out[:, u * HALF : (u + 1) * HALF], res[:])
-
-        layer2(0, 0, own_bf[0], "own", True)
-        layer2(0, 1, z_bf[0], "z", False)
-        store(0)
-        layer2(1, 0, own_bf[1], "own", True)
-        layer2(1, 1, z_bf[1], "z", False)
-        store(1)

@@ -102,8 +102,8 @@ def tile_picked_sagecat_mean_p_kernel(tc, x_words, x_scales, w1, w2, w3, offs, c
         for t in range(1, PACK):
             layer1(t, 0, S, len(PLANE0_PIECES) + t - 1, False)
 
-        w2_tile = shared.tile([P, PACK * N], F32, name="w2_tile", offset=0, align_bytes=ALIGN)
-        w3_tile = keep.tile([P, PACK * N], F32, name="w3_tile")
+        w2_tile = keep.tile([P, PACK * N], F32, name="w2_tile")
+        w3_tile = shared.tile([P, PACK * N], F32, name="w3_tile", offset=ALIGN, align_bytes=ALIGN)
         w2_raw = w2_tile[:]
         w3_raw = w3_tile[:]
         for raw, w in ((w2_raw, w2), (w3_raw, w3)):
@@ -114,10 +114,10 @@ def tile_picked_sagecat_mean_p_kernel(tc, x_words, x_scales, w1, w2, w3, offs, c
         nc.scalar.copy(w23_dst[:, 0], w2_raw.rearrange("p (j c i) -> p c j i", j=PACK, i=RUN))
         nc.scalar.copy(w23_dst[:, 1], w3_raw.rearrange("p (j c i) -> p c j i", j=PACK, i=RUN))
 
-        own = [keep.tile([P, 2, V], F32, name=f"own{pair}") for pair in range(2)]
-        own_bf = keep.tile([P, V * PACK], BF16, name="own_bf", align_bytes=ALIGN)
+        own = keep.tile([P, PACK, V], F32, name="own")
+        own_bf = shared.tile([P, V * PACK], BF16, name="own_bf", offset=2048, align_bytes=ALIGN)
         z_bf = [keep.tile([P, HALF * PACK], BF16, name=f"z_bf{u}", align_bytes=ALIGN) for u in range(2)]
-        held_at = PACK * N * 4
+        held_at = 4096
         nbr = [keep.tile([P, V], F32, name=f"nbr{t}") for t in (0, 1, 3)]
         nbr.insert(2, shared.tile([P, V], F32, name="nbr2", offset=held_at, align_bytes=ALIGN))
 
@@ -126,14 +126,13 @@ def tile_picked_sagecat_mean_p_kernel(tc, x_words, x_scales, w1, w2, w3, offs, c
 
         def gather_first(t):
             nc.vector.tensor_copy(nbr[t][:], h[t][:].indirect(pos_t[0][:]))
-            nc.vector.tensor_copy(own[t // 2][:, t % 2, :], h[t][:].indirect(cen_t[:]))
+
+        def gather_own(t):
+            nc.vector.tensor_copy(own[:, t, :], h[t][:].indirect(cen_t[:]))
 
         def gather_add(t, first, end, total):
             places = pos_t[1][:, first // LIST : end // LIST]
             nc.vector.tensor_tensor(total, h[t][:].indirect(places), nbr[t][:, first:end], ALU.add)
-
-        def round_own(pair):
-            nc.scalar.copy(pair_slots(own_bf[:], pair), own[pair][:].rearrange("p e v -> p v e"))
 
         def round_mean(pair, first, end, total):
             u, at = divmod(first, HALF)
@@ -143,13 +142,18 @@ def tile_picked_sagecat_mean_p_kernel(tc, x_words, x_scales, w1, w2, w3, offs, c
         z_sum = keep.tile([P, 2, V], F32, name="z_sum")
         for t in range(2):
             gather_first(t)
+            gather_own(t)
             gather_add(t, 0, V, z_sum[:, t, :])
-        round_own(0)
         for u in range(2):
             round_mean(0, u * HALF, (u + 1) * HALF, z_sum[:, :, u * HALF : (u + 1) * HALF])
         for t in range(2, PACK):
+            gather_own(t)
+        nc.scalar.copy(
+            own_bf[:].rearrange("p (c i t) -> p c t i", i=RUN, t=PACK),
+            own[:].rearrange("p t (c i) -> p c t i", i=RUN),
+        )
+        for t in range(2, PACK):
             gather_first(t)
-        round_own(1)
         for first, end in LAST_PIECES:
             piece = shared.tile([P, 2, end - first], F32, name=f"piece{first}", offset=first * 8, align_bytes=ALIGN)
             for e in range(2):

@@ -26,7 +26,7 @@ ALIGN = 64
 PLANE0_PIECES = ((0, 256), (256, 384), (384, S))
 PLANE0_PIECE_ON_VECTOR = 1
 
-LAST_PIECES = ((0, 128), (128, 192), (192, V))
+LAST_PIECES = ((0, HALF), (HALF, V))
 
 
 def tile_picked_sagecat_mean_p_kernel(tc, x_words, x_scales, w1, w2, w3, offs, cen, pos1, pos2, out):

@@ -23,10 +23,16 @@ HALF = V // 2
 RUN = 4
 ALIGN = 64
 
+PLANE0_RUNS_ON_SCALAR = 16
+
 PLANE0_PIECES = ((0, 256), (256, 384), (384, S))
 PLANE0_PIECE_ON_VECTOR = 1
 
-LAST_PIECES = ((0, HALF), (HALF, V))
+LAST_PIECES = ((0, 160), (160, V))
+
+W3_AT = 64
+OWN_AT = 2048
+HELD_AT = 4096
 
 
 def tile_picked_sagecat_mean_p_kernel(tc, x_words, x_scales, w1, w2, w3, offs, cen, pos1, pos2, out):
@@ -63,20 +69,22 @@ def tile_picked_sagecat_mean_p_kernel(tc, x_words, x_scales, w1, w2, w3, offs, c
         nc.vector.tensor_copy(x_code[:], word_table[:].bitcast(U32).indirect(offs_t[:]))
         nc.vector.tensor_copy(x_scale[:], scale_table[:].indirect(offs_t[:]))
 
-        w1_bf = [keep.tile([P, P * PACK], BF16, name=f"w1_bf{t}", tag=("w1_bf0", "w1_bf1", "w1_bf0", "w1_bf3")[t], align_bytes=ALIGN) for t in range(PACK)]
-        w1_src = w1_raw[:].rearrange("p (j b t r i) -> p t b r j i", j=PACK, t=PACK, r=2, i=RUN)
+        w1_bf = [
+            keep.tile([P, P * PACK], BF16, name=f"w1_bf{t}", tag=("w1_bf0", "w1_bf1", "w1_bf0", "w1_bf3")[t], align_bytes=ALIGN)
+            for t in range(PACK)
+        ]
+        w1_src = w1_raw[:].rearrange("p (j g t r) -> p t g j r", j=PACK, t=PACK, r=RUN)
         w1_code = [keep.tile([P, P], U32, name=f"w1_code{t}", tag=f"code{t}", align_bytes=ALIGN) for t in range(PACK)]
         w1_scale = [keep.tile([P, P], U8, name=f"w1_scale{t}", tag=f"scale{t}", align_bytes=ALIGN) for t in range(PACK)]
         for t in range(PACK):
-            w1_dst = w1_bf[t][:].rearrange("p (b r i j) -> p b r j i", r=2, i=RUN, j=PACK)
+            w1_dst = w1_bf[t][:].rearrange("p (g r j) -> p g j r", r=RUN, j=PACK)
             if t == 0:
-                for r in range(2):
-                    nc.scalar.activation(w1_dst[:, 0:8, r], w1_src[:, t, 0:8, r], ACT.Copy)
-                nc.vector.tensor_copy(w1_dst[:, 8:16], w1_src[:, t, 8:16])
-            elif t != 2:
-                nc.scalar.copy(w1_dst, w1_src[:, t])
-            else:
+                nc.scalar.activation(w1_dst[:, :PLANE0_RUNS_ON_SCALAR], w1_src[:, t, :PLANE0_RUNS_ON_SCALAR], ACT.Copy)
+                nc.vector.tensor_copy(w1_dst[:, PLANE0_RUNS_ON_SCALAR:], w1_src[:, t, PLANE0_RUNS_ON_SCALAR:])
+            elif t == 2:
                 nc.vector.tensor_copy(w1_dst, w1_src[:, t])
+            else:
+                nc.scalar.copy(w1_dst, w1_src[:, t])
             nc.vector.quantize_mx(out=w1_code[t][:].bitcast(FP8X4), scales=w1_scale[t][:], in_=w1_bf[t][:])
 
         h = [keep.tile([P, S], F32, name=f"h{t}") for t in range(PACK)]
@@ -102,27 +110,21 @@ def tile_picked_sagecat_mean_p_kernel(tc, x_words, x_scales, w1, w2, w3, offs, c
         for t in range(1, PACK):
             layer1(t, 0, S, len(PLANE0_PIECES) + t - 1, False)
 
-        w2_tile = keep.tile([P, PACK * N], F32, name="w2_tile")
-        w3_tile = shared.tile([P, PACK * N], F32, name="w3_tile", offset=ALIGN, align_bytes=ALIGN)
-        w2_raw = w2_tile[:]
-        w3_raw = w3_tile[:]
+        w2_raw = keep.tile([P, PACK * N], F32, name="w2_raw")
+        w3_raw = shared.tile([P, PACK * N], F32, name="w3_raw", offset=W3_AT, align_bytes=ALIGN)
         for raw, w in ((w2_raw, w2), (w3_raw, w3)):
             for t in range(PACK):
-                nc.sync.dma_start(raw[:, t * N : (t + 1) * N], w.rearrange("(b t r) n -> t b r n", t=PACK, r=8)[t])
+                nc.sync.dma_start(raw[:, t * N : (t + 1) * N], w.rearrange("(g t r) n -> t g r n", t=PACK, r=RUN)[t])
         w23_bf = keep.tile([P, 2 * N * PACK], BF16, name="w23_bf", tag=f"scale{PACK - 1}", align_bytes=ALIGN)
-        w23_dst = w23_bf[:].rearrange("p (w c i j) -> p w c j i", w=2, i=RUN, j=PACK)
-        nc.scalar.copy(w23_dst[:, 0], w2_raw.rearrange("p (j c i) -> p c j i", j=PACK, i=RUN))
-        nc.scalar.copy(w23_dst[:, 1], w3_raw.rearrange("p (j c i) -> p c j i", j=PACK, i=RUN))
+        w23_dst = w23_bf[:].rearrange("p (w c i t) -> p w c t i", w=2, i=RUN, t=PACK)
+        for index, raw in enumerate((w2_raw, w3_raw)):
+            nc.scalar.copy(w23_dst[:, index], raw[:].rearrange("p (t c i) -> p c t i", t=PACK, i=RUN))
 
         own = keep.tile([P, PACK, V], F32, name="own")
-        own_bf = shared.tile([P, V * PACK], BF16, name="own_bf", offset=2048, align_bytes=ALIGN)
-        z_bf = [keep.tile([P, HALF * PACK], BF16, name=f"z_bf{u}", align_bytes=ALIGN) for u in range(2)]
-        held_at = 4096
+        own_bf = shared.tile([P, V * PACK], BF16, name="own_bf", offset=OWN_AT, align_bytes=ALIGN)
+        z_bf = keep.tile([P, V * PACK], BF16, name="z_bf", align_bytes=ALIGN)
         nbr = [keep.tile([P, V], F32, name=f"nbr{t}") for t in (0, 1, 3)]
-        nbr.insert(2, shared.tile([P, V], F32, name="nbr2", offset=held_at, align_bytes=ALIGN))
-
-        def pair_slots(values, pair):
-            return values.rearrange("p (v g e) -> p g v e", g=2, e=2)[:, pair]
+        nbr.insert(2, shared.tile([P, V], F32, name="nbr2", offset=HELD_AT, align_bytes=ALIGN))
 
         def gather_first(t):
             nc.vector.tensor_copy(nbr[t][:], h[t][:].indirect(pos_t[0][:]))
@@ -135,8 +137,7 @@ def tile_picked_sagecat_mean_p_kernel(tc, x_words, x_scales, w1, w2, w3, offs, c
             nc.vector.tensor_tensor(total, h[t][:].indirect(places), nbr[t][:, first:end], ALU.add)
 
         def round_mean(pair, first, end, total):
-            u, at = divmod(first, HALF)
-            slots = pair_slots(z_bf[u][:, at * PACK : (at + end - first) * PACK], pair)
+            slots = z_bf[:, first * PACK : end * PACK].rearrange("p (v g e) -> p g v e", g=2, e=2)[:, pair]
             nc.scalar.activation(slots, total.rearrange("p e v -> p v e"), ACT.Copy, scale=0.5)
 
         z_sum = keep.tile([P, 2, V], F32, name="z_sum")
@@ -144,8 +145,9 @@ def tile_picked_sagecat_mean_p_kernel(tc, x_words, x_scales, w1, w2, w3, offs, c
             gather_first(t)
             gather_own(t)
             gather_add(t, 0, V, z_sum[:, t, :])
-        for u in range(2):
-            round_mean(0, u * HALF, (u + 1) * HALF, z_sum[:, :, u * HALF : (u + 1) * HALF])
+        for first in (0, HALF):
+            round_mean(0, first, first + HALF, z_sum[:, :, first : first + HALF])
+
         for t in range(2, PACK):
             gather_own(t)
         nc.scalar.copy(
@@ -155,36 +157,36 @@ def tile_picked_sagecat_mean_p_kernel(tc, x_words, x_scales, w1, w2, w3, offs, c
         for t in range(2, PACK):
             gather_first(t)
         for first, end in LAST_PIECES:
-            piece = shared.tile([P, 2, end - first], F32, name=f"piece{first}", offset=first * 8, align_bytes=ALIGN)
+            sums = shared.tile([P, 2, end - first], F32, name=f"sums{first}", offset=first * 8, align_bytes=ALIGN)
             for e in range(2):
-                gather_add(2 + e, first, end, piece[:, e, :])
-            round_mean(1, first, end, piece[:])
+                gather_add(2 + e, first, end, sums[:, e, :])
+            round_mean(1, first, end, sums[:])
 
-        def quantize(name, values, slot):
+        def quantize(name, values, place):
             code = keep.tile([P, HALF], U32, name=f"{name}_code", align_bytes=ALIGN)
-            scale = shared.tile([P, HALF], U8, name=f"{name}_scale", offset=held_at + slot * HALF, align_bytes=ALIGN)
+            scale = shared.tile([P, HALF], U8, name=f"{name}_scale", offset=HELD_AT + place * HALF, align_bytes=ALIGN)
             nc.vector.quantize_mx(out=code[:].bitcast(FP8X4), scales=scale[:], in_=values)
             return code, scale
 
         acc_out = [psum.tile([P, HALF], F32, name=f"acc_out{u}") for u in range(2)]
 
-        def layer2(u, weights, values, first):
+        def layer2(u, weights, values, opens):
             nc.tensor.matmul_mx(
                 out=acc_out[u][:],
                 lhsT=weights[0][:].bitcast(FP8X4),
                 lhsT_scale=weights[1][:],
                 rhs=values[0][:].bitcast(FP8X4),
                 rhs_scale=values[1][:],
-                start=first,
-                stop=not first,
+                start=opens,
+                stop=not opens,
             )
 
-        w2_mx = quantize("w2", w23_bf[:, 0 : N * PACK], 0)
+        w2_mx = quantize("w2", w23_bf[:, : N * PACK], 0)
+        w3_mx = quantize("w3", w23_bf[:, N * PACK :], 1)
         for u in range(2):
-            layer2(u, w2_mx, quantize(f"own{u}", own_bf[:, u * HALF * PACK : (u + 1) * HALF * PACK], 1 + u), True)
-        w3_mx = quantize("w3", w23_bf[:, N * PACK :], 3)
-        for u in range(2):
-            layer2(u, w3_mx, quantize(f"z{u}", z_bf[u][:], 4 + u), False)
+            group = slice(u * HALF * PACK, (u + 1) * HALF * PACK)
+            layer2(u, w2_mx, quantize(f"own{u}", own_bf[:, group], 2 + 2 * u), True)
+            layer2(u, w3_mx, quantize(f"z{u}", z_bf[:, group], 3 + 2 * u), False)
             res = keep.tile([P, HALF], F32, name=f"res{u}")
             nc.scalar.copy(res[:], acc_out[u][:])
             nc.sync.dma_start(out[:, u * HALF : (u + 1) * HALF], res[:])

@@ -30,9 +30,10 @@ PLANE0_PIECE_ON_VECTOR = 1
 
 LAST_PIECES = ((0, 160), (160, V))
 
-W3_AT = 64
-OWN_AT = 2048
-HELD_AT = 4096
+SUMS_AT = 2048
+W3_AT = 2112
+OWN_AT = 4096
+HELD_AT = 6144
 
 
 def tile_picked_sagecat_mean_p_kernel(tc, x_words, x_scales, w1, w2, w3, offs, cen, pos1, pos2, out):
@@ -48,7 +49,7 @@ def tile_picked_sagecat_mean_p_kernel(tc, x_words, x_scales, w1, w2, w3, offs, c
         pos_t = [lists.tile([P, V // LIST], U16, name=f"pos_t{d}") for d in range(2)]
 
         scale_table = keep.tile([P, T], U8, name="scale_table", align_bytes=ALIGN)
-        word_table = keep.tile([P, T], I32, name="word_table", align_bytes=ALIGN)
+        word_table = shared.tile([P, T], I32, name="word_table", offset=0, align_bytes=ALIGN)
         nc.vector.memset(scale_table[:].bitcast(I32), 0)
 
         w1_raw = keep.tile([P, PACK * H], F32, name="w1_raw")
@@ -110,7 +111,7 @@ def tile_picked_sagecat_mean_p_kernel(tc, x_words, x_scales, w1, w2, w3, offs, c
         for t in range(1, PACK):
             layer1(t, 0, S, len(PLANE0_PIECES) + t - 1, False)
 
-        w2_raw = keep.tile([P, PACK * N], F32, name="w2_raw")
+        w2_raw = shared.tile([P, PACK * N], F32, name="w2_raw", offset=0, align_bytes=ALIGN)
         w3_raw = shared.tile([P, PACK * N], F32, name="w3_raw", offset=W3_AT, align_bytes=ALIGN)
         for raw, w in ((w2_raw, w2), (w3_raw, w3)):
             for t in range(PACK):
@@ -157,7 +158,7 @@ def tile_picked_sagecat_mean_p_kernel(tc, x_words, x_scales, w1, w2, w3, offs, c
         for t in range(2, PACK):
             gather_first(t)
         for first, end in LAST_PIECES:
-            sums = shared.tile([P, 2, end - first], F32, name=f"sums{first}", offset=first * 8, align_bytes=ALIGN)
+            sums = shared.tile([P, 2, end - first], F32, name=f"sums{first}", offset=SUMS_AT + first * 8, align_bytes=ALIGN)
             for e in range(2):
                 gather_add(2 + e, first, end, sums[:, e, :])
             round_mean(1, first, end, sums[:])

@@ -24,11 +24,13 @@ RUN = 4
 ALIGN = 64
 
 PLANE0_RUNS_ON_SCALAR = 16
+PLANE2_RUNS_ON_VECTOR = 24
 
 PLANE0_PIECES = ((0, 256), (256, 384), (384, S))
 PLANE0_PIECE_ON_VECTOR = 1
 
 LAST_PIECES = ((0, 160), (160, V))
+LAST_CALL = 192
 
 SUMS_AT = 2048
 W3_AT = 2112
@@ -62,6 +64,13 @@ def tile_picked_sagecat_mean_p_kernel(tc, x_words, x_scales, w1, w2, w3, offs, c
                 x_scales[0, PACK * q : PACK * (q + 1), :].bitcast(I32),
             )
         nc.sync.dma_start(w1_raw[:], w1.rearrange("(p j) c -> p (j c)", j=PACK))
+
+        def load_slots(raw, w):
+            for t in range(PACK):
+                nc.sync.dma_start(raw[:, t * N : (t + 1) * N], w.rearrange("(g t r) n -> t g r n", t=PACK, r=RUN)[t])
+
+        w2_raw = keep.tile([P, PACK * N], F32, name="w2_raw")
+        load_slots(w2_raw, w2)
         nc.sync.dma_start(pos_t[0][:], pos1)
         nc.sync.dma_start(pos_t[1][:], pos2)
 
@@ -71,22 +80,28 @@ def tile_picked_sagecat_mean_p_kernel(tc, x_words, x_scales, w1, w2, w3, offs, c
         nc.vector.tensor_copy(x_scale[:], scale_table[:].indirect(offs_t[:]))
 
         w1_bf = [
-            keep.tile([P, P * PACK], BF16, name=f"w1_bf{t}", tag=("w1_bf0", "w1_bf1", "w1_bf0", "w1_bf3")[t], align_bytes=ALIGN)
+            keep.tile([P, P * PACK], BF16, name=f"w1_bf{t}", align_bytes=ALIGN)
             for t in range(PACK)
         ]
         w1_src = w1_raw[:].rearrange("p (j g t r) -> p t g j r", j=PACK, t=PACK, r=RUN)
         w1_code = [keep.tile([P, P], U32, name=f"w1_code{t}", tag=f"code{t}", align_bytes=ALIGN) for t in range(PACK)]
         w1_scale = [keep.tile([P, P], U8, name=f"w1_scale{t}", tag=f"scale{t}", align_bytes=ALIGN) for t in range(PACK)]
+        w1_dst = [bf[:].rearrange("p (g r j) -> p g j r", r=RUN, j=PACK) for bf in w1_bf]
+        nc.scalar.activation(w1_dst[0][:, :PLANE0_RUNS_ON_SCALAR], w1_src[:, 0, :PLANE0_RUNS_ON_SCALAR], ACT.Copy)
+        nc.vector.tensor_copy(w1_dst[0][:, PLANE0_RUNS_ON_SCALAR:], w1_src[:, 0, PLANE0_RUNS_ON_SCALAR:])
+        nc.vector.tensor_copy(w1_dst[2][:, :PLANE2_RUNS_ON_VECTOR], w1_src[:, 2, :PLANE2_RUNS_ON_VECTOR])
+        nc.scalar.copy(w1_dst[1], w1_src[:, 1])
+        nc.scalar.copy(w1_dst[2][:, PLANE2_RUNS_ON_VECTOR:], w1_src[:, 2, PLANE2_RUNS_ON_VECTOR:])
+        nc.scalar.copy(w1_dst[3], w1_src[:, 3])
         for t in range(PACK):
-            w1_dst = w1_bf[t][:].rearrange("p (g r j) -> p g j r", r=RUN, j=PACK)
-            if t == 0:
-                nc.scalar.activation(w1_dst[:, :PLANE0_RUNS_ON_SCALAR], w1_src[:, t, :PLANE0_RUNS_ON_SCALAR], ACT.Copy)
-                nc.vector.tensor_copy(w1_dst[:, PLANE0_RUNS_ON_SCALAR:], w1_src[:, t, PLANE0_RUNS_ON_SCALAR:])
-            elif t == 2:
-                nc.vector.tensor_copy(w1_dst, w1_src[:, t])
-            else:
-                nc.scalar.copy(w1_dst, w1_src[:, t])
             nc.vector.quantize_mx(out=w1_code[t][:].bitcast(FP8X4), scales=w1_scale[t][:], in_=w1_bf[t][:])
+
+        def slots_last(bf, raw):
+            return bf[:].rearrange("p (c i t) -> p c t i", i=RUN, t=PACK), raw[:].rearrange("p (t c i) -> p c t i", t=PACK, i=RUN)
+
+        w2_bf = keep.tile([P, N * PACK], BF16, name="w2_bf", align_bytes=ALIGN)
+        w2_mx = (keep.tile([P, N], U32, name="w2_code", align_bytes=ALIGN), keep.tile([P, N], U8, name="w2_scale", align_bytes=ALIGN))
+        nc.vector.tensor_copy(*slots_last(w2_bf, w2_raw))
 
         h = [keep.tile([P, S], F32, name=f"h{t}") for t in range(PACK)]
 
@@ -108,18 +123,14 @@ def tile_picked_sagecat_mean_p_kernel(tc, x_words, x_scales, w1, w2, w3, offs, c
 
         for piece, (first, end) in enumerate(PLANE0_PIECES):
             layer1(0, first, end, piece, piece == PLANE0_PIECE_ON_VECTOR)
+        nc.vector.quantize_mx(out=w2_mx[0][:].bitcast(FP8X4), scales=w2_mx[1][:], in_=w2_bf[:])
         for t in range(1, PACK):
             layer1(t, 0, S, len(PLANE0_PIECES) + t - 1, False)
 
-        w2_raw = shared.tile([P, PACK * N], F32, name="w2_raw", offset=0, align_bytes=ALIGN)
         w3_raw = shared.tile([P, PACK * N], F32, name="w3_raw", offset=W3_AT, align_bytes=ALIGN)
-        for raw, w in ((w2_raw, w2), (w3_raw, w3)):
-            for t in range(PACK):
-                nc.sync.dma_start(raw[:, t * N : (t + 1) * N], w.rearrange("(g t r) n -> t g r n", t=PACK, r=RUN)[t])
-        w23_bf = keep.tile([P, 2 * N * PACK], BF16, name="w23_bf", tag=f"scale{PACK - 1}", align_bytes=ALIGN)
-        w23_dst = w23_bf[:].rearrange("p (w c i t) -> p w c t i", w=2, i=RUN, t=PACK)
-        for index, raw in enumerate((w2_raw, w3_raw)):
-            nc.scalar.copy(w23_dst[:, index], raw[:].rearrange("p (t c i) -> p c t i", t=PACK, i=RUN))
+        load_slots(w3_raw, w3)
+        w3_bf = keep.tile([P, N * PACK], BF16, name="w3_bf", tag=f"scale{PACK - 1}", align_bytes=ALIGN)
+        nc.scalar.copy(*slots_last(w3_bf, w3_raw))
 
         own = keep.tile([P, PACK, V], F32, name="own")
         own_bf = shared.tile([P, V * PACK], BF16, name="own_bf", offset=OWN_AT, align_bytes=ALIGN)
@@ -161,12 +172,17 @@ def tile_picked_sagecat_mean_p_kernel(tc, x_words, x_scales, w1, w2, w3, offs, c
             sums = shared.tile([P, 2, end - first], F32, name=f"sums{first}", offset=SUMS_AT + first * 8, align_bytes=ALIGN)
             for e in range(2):
                 gather_add(2 + e, first, end, sums[:, e, :])
-            round_mean(1, first, end, sums[:])
+            for cut, cut_end in ((first, min(end, LAST_CALL)), (max(first, LAST_CALL), end)):
+                if cut < cut_end:
+                    round_mean(1, cut, cut_end, sums[:, :, cut - first : cut_end - first])
 
-        def quantize(name, values, place):
+        def quantize(name, values, place, cuts=(0, HALF)):
             code = keep.tile([P, HALF], U32, name=f"{name}_code", align_bytes=ALIGN)
             scale = shared.tile([P, HALF], U8, name=f"{name}_scale", offset=HELD_AT + place * HALF, align_bytes=ALIGN)
-            nc.vector.quantize_mx(out=code[:].bitcast(FP8X4), scales=scale[:], in_=values)
+            for first, end in zip(cuts, cuts[1:]):
+                nc.vector.quantize_mx(
+                    out=code[:, first:end].bitcast(FP8X4), scales=scale[:, first:end], in_=values[:, first * PACK : end * PACK]
+                )
             return code, scale
 
         acc_out = [psum.tile([P, HALF], F32, name=f"acc_out{u}") for u in range(2)]
@@ -182,12 +198,11 @@ def tile_picked_sagecat_mean_p_kernel(tc, x_words, x_scales, w1, w2, w3, offs, c
                 stop=not opens,
             )
 
-        w2_mx = quantize("w2", w23_bf[:, : N * PACK], 0)
-        w3_mx = quantize("w3", w23_bf[:, N * PACK :], 1)
+        w3_mx = quantize("w3", w3_bf[:], 1)
         for u in range(2):
             group = slice(u * HALF * PACK, (u + 1) * HALF * PACK)
             layer2(u, w2_mx, quantize(f"own{u}", own_bf[:, group], 2 + 2 * u), True)
-            layer2(u, w3_mx, quantize(f"z{u}", z_bf[:, group], 3 + 2 * u), False)
+            layer2(u, w3_mx, quantize(f"z{u}", z_bf[:, group], 3 + 2 * u, ((0, HALF), (0, LAST_CALL - HALF, HALF))[u]), False)
             res = keep.tile([P, HALF], F32, name=f"res{u}")
             nc.scalar.copy(res[:], acc_out[u][:])
             nc.sync.dma_start(out[:, u * HALF : (u + 1) * HALF], res[:])

@@ -20,11 +20,11 @@ PACK = 4
 QUADRANT = 32
 LIST = 16
 HALF = V // 2
-RUN = 4
+RUN = 2
 ALIGN = 64
 
-PLANE0_RUNS_ON_SCALAR = 16
-PLANE2_RUNS_ON_VECTOR = 24
+PLANE0_RUNS_ON_SCALAR = 32
+PLANE2_RUNS_ON_VECTOR = 48
 
 PLANE0_PIECES = ((0, 256), (256, 384), (384, S))
 PLANE0_PIECE_ON_VECTOR = 1
@@ -66,12 +66,13 @@ def tile_picked_sagecat_mean_p_kernel(tc, x_words, x_scales, w1, w2, w3, offs, c
         nc.sync.dma_start(w1_raw[:], w1.rearrange("(p j) c -> p (j c)", j=PACK))
 
         def load_slots(raw, w):
-            for t in range(PACK):
-                nc.sync.dma_start(raw[:, t * N : (t + 1) * N], w.rearrange("(g t r) n -> t g r n", t=PACK, r=RUN)[t])
+            rows = w.rearrange("(g t r) n -> r g t n", t=PACK, r=RUN)
+            for r in range(RUN):
+                nc.sync.dma_start(raw[r:P:RUN, :].rearrange("g (t n) -> g t n", t=PACK), rows[r])
 
         w2_raw = keep.tile([P, PACK * N], F32, name="w2_raw")
-        load_slots(w2_raw, w2)
         nc.sync.dma_start(pos_t[0][:], pos1)
+        load_slots(w2_raw, w2)
         nc.sync.dma_start(pos_t[1][:], pos2)
 
         x_code = keep.tile([P, S], U32, name="x_code", align_bytes=ALIGN)
@@ -99,7 +100,7 @@ def tile_picked_sagecat_mean_p_kernel(tc, x_words, x_scales, w1, w2, w3, offs, c
         def slots_last(bf, raw):
             return bf[:].rearrange("p (c i t) -> p c t i", i=RUN, t=PACK), raw[:].rearrange("p (t c i) -> p c t i", t=PACK, i=RUN)
 
-        w2_bf = keep.tile([P, N * PACK], BF16, name="w2_bf", align_bytes=ALIGN)
+        w2_bf = keep.tile([P, N * PACK], BF16, name="w2_bf", tag="w1_bf0", align_bytes=ALIGN)
         w2_mx = (keep.tile([P, N], U32, name="w2_code", align_bytes=ALIGN), keep.tile([P, N], U8, name="w2_scale", align_bytes=ALIGN))
         nc.vector.tensor_copy(*slots_last(w2_bf, w2_raw))
 

@@ -29,14 +29,6 @@ PLANE2_RUNS_ON_VECTOR = 48
 PLANE0_PIECES = ((0, 256), (256, 384), (384, S))
 PLANE0_PIECE_ON_VECTOR = 1
 
-LAST_PIECES = ((0, 160), (160, V))
-LAST_CALL = 192
-
-SUMS_AT = 2048
-W3_AT = 2112
-OWN_AT = 4096
-HELD_AT = 6144
-
 
 def tile_picked_sagecat_mean_p_kernel(tc, x_words, x_scales, w1, w2, w3, offs, cen, pos1, pos2, out):
     nc = tc.nc
@@ -125,66 +117,42 @@ def tile_picked_sagecat_mean_p_kernel(tc, x_words, x_scales, w1, w2, w3, offs, c
         for piece, (first, end) in enumerate(PLANE0_PIECES):
             layer1(0, first, end, piece, piece == PLANE0_PIECE_ON_VECTOR)
         nc.vector.quantize_mx(out=w2_mx[0][:].bitcast(FP8X4), scales=w2_mx[1][:], in_=w2_bf[:])
-        for t in range(1, PACK):
-            layer1(t, 0, S, len(PLANE0_PIECES) + t - 1, False)
 
-        w3_raw = shared.tile([P, PACK * N], F32, name="w3_raw", offset=W3_AT, align_bytes=ALIGN)
+        w3_raw = shared.tile([P, PACK * N], F32, name="w3_raw", offset=0, align_bytes=ALIGN)
         load_slots(w3_raw, w3)
-        w3_bf = keep.tile([P, N * PACK], BF16, name="w3_bf", tag=f"scale{PACK - 1}", align_bytes=ALIGN)
-        nc.scalar.copy(*slots_last(w3_bf, w3_raw))
 
         own = keep.tile([P, PACK, V], F32, name="own")
-        own_bf = shared.tile([P, V * PACK], BF16, name="own_bf", offset=OWN_AT, align_bytes=ALIGN)
+        z_sum = keep.tile([P, PACK, V], F32, name="z_sum")
+        own_bf = keep.tile([P, V * PACK], BF16, name="own_bf", align_bytes=ALIGN)
         z_bf = keep.tile([P, V * PACK], BF16, name="z_bf", align_bytes=ALIGN)
-        nbr = [keep.tile([P, V], F32, name=f"nbr{t}") for t in (0, 1, 3)]
-        nbr.insert(2, shared.tile([P, V], F32, name="nbr2", offset=HELD_AT, align_bytes=ALIGN))
+        nbr = [keep.tile([P, V], F32, name=f"nbr{t}") for t in range(PACK)]
 
-        def gather_first(t):
-            nc.vector.tensor_copy(nbr[t][:], h[t][:].indirect(pos_t[0][:]))
-
-        def gather_own(t):
-            nc.vector.tensor_copy(own[:, t, :], h[t][:].indirect(cen_t[:]))
-
-        def gather_add(t, first, end, total):
-            places = pos_t[1][:, first // LIST : end // LIST]
-            nc.vector.tensor_tensor(total, h[t][:].indirect(places), nbr[t][:, first:end], ALU.add)
-
-        def round_mean(pair, first, end, total):
-            slots = z_bf[:, first * PACK : end * PACK].rearrange("p (v g e) -> p g v e", g=2, e=2)[:, pair]
-            nc.scalar.activation(slots, total.rearrange("p e v -> p v e"), ACT.Copy, scale=0.5)
-
-        z_sum = keep.tile([P, 2, V], F32, name="z_sum")
-        for t in range(2):
-            gather_first(t)
-            gather_own(t)
-            gather_add(t, 0, V, z_sum[:, t, :])
-        for first in (0, HALF):
-            round_mean(0, first, first + HALF, z_sum[:, :, first : first + HALF])
-
-        for t in range(2, PACK):
-            gather_own(t)
-        nc.scalar.copy(
-            own_bf[:].rearrange("p (c i t) -> p c t i", i=RUN, t=PACK),
-            own[:].rearrange("p t (c i) -> p c t i", i=RUN),
-        )
-        for t in range(2, PACK):
-            gather_first(t)
-        for first, end in LAST_PIECES:
-            sums = shared.tile([P, 2, end - first], F32, name=f"sums{first}", offset=SUMS_AT + first * 8, align_bytes=ALIGN)
-            for e in range(2):
-                gather_add(2 + e, first, end, sums[:, e, :])
-            for cut, cut_end in ((first, min(end, LAST_CALL)), (max(first, LAST_CALL), end)):
-                if cut < cut_end:
-                    round_mean(1, cut, cut_end, sums[:, :, cut - first : cut_end - first])
-
-        def quantize(name, values, place, cuts=(0, HALF)):
+        def quantize(name, values):
             code = keep.tile([P, HALF], U32, name=f"{name}_code", align_bytes=ALIGN)
-            scale = shared.tile([P, HALF], U8, name=f"{name}_scale", offset=HELD_AT + place * HALF, align_bytes=ALIGN)
-            for first, end in zip(cuts, cuts[1:]):
-                nc.vector.quantize_mx(
-                    out=code[:, first:end].bitcast(FP8X4), scales=scale[:, first:end], in_=values[:, first * PACK : end * PACK]
-                )
+            scale = keep.tile([P, HALF], U8, name=f"{name}_scale", align_bytes=ALIGN)
+            nc.vector.quantize_mx(out=code[:].bitcast(FP8X4), scales=scale[:], in_=values)
             return code, scale
+
+        for t in range(PACK):
+            if t + 1 < PACK:
+                layer1(t + 1, 0, S, len(PLANE0_PIECES) + t, True)
+            else:
+                w3_bf = keep.tile([P, N * PACK], BF16, name="w3_bf", tag=f"scale{PACK - 1}", align_bytes=ALIGN)
+                nc.vector.tensor_copy(*slots_last(w3_bf, w3_raw))
+            nc.scalar.activation(nbr[t][:], h[t][:].indirect(pos_t[0][:]), ACT.Copy)
+            nc.scalar.activation(own[:, t, :], h[t][:].indirect(cen_t[:]), ACT.Copy)
+            nc.vector.tensor_tensor(z_sum[:, t, :], h[t][:].indirect(pos_t[1][:]), nbr[t][:], ALU.add)
+        w3_mx = quantize("w3", w3_bf[:])
+
+        def interleaved(bf, planes, u):
+            return (
+                bf[:, u * HALF * PACK : (u + 1) * HALF * PACK].rearrange("p (c i t) -> p c t i", i=RUN, t=PACK),
+                planes[:, :, u * HALF : (u + 1) * HALF].rearrange("p t (c i) -> p c t i", i=RUN),
+            )
+
+        for u in range(2):
+            nc.vector.tensor_scalar(*interleaved(z_bf, z_sum, u), 0.5, None, ALU.mult)
+            nc.scalar.copy(*interleaved(own_bf, own, u))
 
         acc_out = [psum.tile([P, HALF], F32, name=f"acc_out{u}") for u in range(2)]
 
@@ -199,11 +167,11 @@ def tile_picked_sagecat_mean_p_kernel(tc, x_words, x_scales, w1, w2, w3, offs, c
                 stop=not opens,
             )
 
-        w3_mx = quantize("w3", w3_bf[:], 1)
+        groups = [slice(u * HALF * PACK, (u + 1) * HALF * PACK) for u in range(2)]
         for u in range(2):
-            group = slice(u * HALF * PACK, (u + 1) * HALF * PACK)
-            layer2(u, w2_mx, quantize(f"own{u}", own_bf[:, group], 2 + 2 * u), True)
-            layer2(u, w3_mx, quantize(f"z{u}", z_bf[:, group], 3 + 2 * u, ((0, HALF), (0, LAST_CALL - HALF, HALF))[u]), False)
+            layer2(u, w3_mx, quantize(f"z{u}", z_bf[:, groups[u]]), True)
+        for u in range(2):
+            layer2(u, w2_mx, quantize(f"own{u}", own_bf[:, groups[u]]), False)
             res = keep.tile([P, HALF], F32, name=f"res{u}")
             nc.scalar.copy(res[:], acc_out[u][:])
             nc.sync.dma_start(out[:, u * HALF : (u + 1) * HALF], res[:])

from contextlib import ExitStack

import concourse.mybir as mybir

K, T, S, V, H, N = 512, 1024, 512, 256, 512, 128
FLOPS = 2 * K * S * H + 2 * 2 * H * V * N

F32 = mybir.dt.float32
BF16 = mybir.dt.bfloat16
I32 = mybir.dt.int32
U32 = mybir.dt.uint32
U16 = mybir.dt.uint16
U8 = mybir.dt.uint8
FP8X4 = mybir.dt.float8_e4m3fn_x4
ACT = mybir.ActivationFunctionType
ALU = mybir.AluOpType

P = 128
PACK = 4
QUADRANT = 32
LIST = 16
HALF = V // 2
RUN = 2
ALIGN = 64

PLANE0_RUNS_ON_SCALAR = 32
PLANE2_RUNS_ON_VECTOR = 48

PLANE0_PIECES = ((0, 256), (256, 384), (384, S))
PLANE0_PIECE_ON_VECTOR = 1


def tile_picked_sagecat_mean_p_kernel(tc, x_words, x_scales, w1, w2, w3, offs, cen, pos1, pos2, out):
    nc = tc.nc
    with ExitStack() as ctx:
        lists = ctx.enter_context(tc.tile_pool(name="lists", bufs=1))
        keep = ctx.enter_context(tc.tile_pool(name="keep", bufs=1))
        shared = ctx.enter_context(tc.tile_pool(name="shared", bufs=1))
        psum = ctx.enter_context(tc.psum_pool(name="psum", bufs=1))

        offs_t = lists.tile([P, S // LIST], U16, name="offs_t")
        cen_t = lists.tile([P, V // LIST], U16, name="cen_t")
        pos_t = [lists.tile([P, V // LIST], U16, name=f"pos_t{d}") for d in range(2)]

        scale_table = keep.tile([P, T], U8, name="scale_table", align_bytes=ALIGN)
        word_table = shared.tile([P, T], I32, name="word_table", offset=0, align_bytes=ALIGN)
        nc.vector.memset(scale_table[:].bitcast(I32), 0)

        w1_raw = keep.tile([P, PACK * H], F32, name="w1_raw")
        nc.sync.dma_start(word_table[:], x_words[0].rearrange("p n t -> p (n t)").bitcast(I32))
        nc.sync.dma_start(offs_t[:], offs)
        nc.sync.dma_start(cen_t[:], cen)
        for q in range(P // QUADRANT):
            nc.sync.dma_start(
                scale_table[QUADRANT * q : QUADRANT * q + PACK, :].bitcast(I32),
                x_scales[0, PACK * q : PACK * (q + 1), :].bitcast(I32),
            )
        nc.sync.dma_start(w1_raw[:], w1.rearrange("(p j) c -> p (j c)", j=PACK))

        def load_slots(raw, w):
            rows = w.rearrange("(g t r) n -> r g t n", t=PACK, r=RUN)
            for r in range(RUN):
                nc.sync.dma_start(raw[r:P:RUN, :].rearrange("g (t n) -> g t n", t=PACK), rows[r])

        w2_raw = keep.tile([P, PACK * N], F32, name="w2_raw")
        nc.sync.dma_start(pos_t[0][:], pos1)
        load_slots(w2_raw, w2)
        nc.sync.dma_start(pos_t[1][:], pos2)

        x_code = keep.tile([P, S], U32, name="x_code", align_bytes=ALIGN)
        x_scale = keep.tile([P, S], U8, name="x_scale", align_bytes=ALIGN)
        nc.vector.tensor_copy(x_code[:], word_table[:].bitcast(U32).indirect(offs_t[:]))
        nc.vector.tensor_copy(x_scale[:], scale_table[:].indirect(offs_t[:]))

        w1_bf = [
            keep.tile([P, P * PACK], BF16, name=f"w1_bf{t}", align_bytes=ALIGN)
            for t in range(PACK)
        ]
        w1_src = w1_raw[:].rearrange("p (j g t r) -> p t g j r", j=PACK, t=PACK, r=RUN)
        w1_code = [keep.tile([P, P], U32, name=f"w1_code{t}", tag=f"code{t}", align_bytes=ALIGN) for t in range(PACK)]
        w1_scale = [keep.tile([P, P], U8, name=f"w1_scale{t}", tag=f"scale{t}", align_bytes=ALIGN) for t in range(PACK)]
        w1_dst = [bf[:].rearrange("p (g r j) -> p g j r", r=RUN, j=PACK) for bf in w1_bf]
        nc.scalar.activation(w1_dst[0][:, :PLANE0_RUNS_ON_SCALAR], w1_src[:, 0, :PLANE0_RUNS_ON_SCALAR], ACT.Copy)
        nc.vector.tensor_copy(w1_dst[0][:, PLANE0_RUNS_ON_SCALAR:], w1_src[:, 0, PLANE0_RUNS_ON_SCALAR:])
        nc.vector.tensor_copy(w1_dst[2][:, :PLANE2_RUNS_ON_VECTOR], w1_src[:, 2, :PLANE2_RUNS_ON_VECTOR])
        nc.scalar.copy(w1_dst[1], w1_src[:, 1])
        nc.scalar.copy(w1_dst[2][:, PLANE2_RUNS_ON_VECTOR:], w1_src[:, 2, PLANE2_RUNS_ON_VECTOR:])
        nc.scalar.copy(w1_dst[3], w1_src[:, 3])
        for t in range(PACK):
            nc.vector.quantize_mx(out=w1_code[t][:].bitcast(FP8X4), scales=w1_scale[t][:], in_=w1_bf[t][:])

        def slots_last(bf, raw):
            return bf[:].rearrange("p (c i t) -> p c t i", i=RUN, t=PACK), raw[:].rearrange("p (t c i) -> p c t i", t=PACK, i=RUN)

        w2_bf = keep.tile([P, N * PACK], BF16, name="w2_bf", tag="w1_bf0", align_bytes=ALIGN)
        w2_mx = (keep.tile([P, N], U32, name="w2_code", align_bytes=ALIGN), keep.tile([P, N], U8, name="w2_scale", align_bytes=ALIGN))
        nc.vector.tensor_copy(*slots_last(w2_bf, w2_raw))

        h = [keep.tile([P, S], F32, name=f"h{t}") for t in range(PACK)]

        def layer1(t, first, end, bank, on_vector):
            acc = psum.tile([P, end - first], F32, name="acc", tag=f"bank{bank}")
            nc.tensor.matmul_mx(
                out=acc[:],
                lhsT=w1_code[t][:].bitcast(FP8X4),
                lhsT_scale=w1_scale[t][:],
                rhs=x_code[:, first:end].bitcast(FP8X4),
                rhs_scale=x_scale[:, first:end],
                start=True,
                stop=True,
            )
            if on_vector:
                nc.vector.tensor_scalar(h[t][:, first:end], acc[:], 0.0, None, ALU.max)
            else:
                nc.scalar.activation(h[t][:, first:end], acc[:], ACT.Relu)

        for piece, (first, end) in enumerate(PLANE0_PIECES):
            layer1(0, first, end, piece, piece == PLANE0_PIECE_ON_VECTOR)
        nc.vector.quantize_mx(out=w2_mx[0][:].bitcast(FP8X4), scales=w2_mx[1][:], in_=w2_bf[:])

        w3_raw = shared.tile([P, PACK * N], F32, name="w3_raw", offset=0, align_bytes=ALIGN)
        load_slots(w3_raw, w3)

        own = keep.tile([P, PACK, V], F32, name="own")
        z_sum = keep.tile([P, PACK, V], F32, name="z_sum")
        own_bf = keep.tile([P, V * PACK], BF16, name="own_bf", align_bytes=ALIGN)
        z_bf = keep.tile([P, V * PACK], BF16, name="z_bf", align_bytes=ALIGN)
        nbr = [keep.tile([P, V], F32, name=f"nbr{t}") for t in range(PACK)]

        def quantize(name, values):
            code = keep.tile([P, HALF], U32, name=f"{name}_code", align_bytes=ALIGN)
            scale = keep.tile([P, HALF], U8, name=f"{name}_scale", align_bytes=ALIGN)
            nc.vector.quantize_mx(out=code[:].bitcast(FP8X4), scales=scale[:], in_=values)
            return code, scale

        for t in range(PACK):
            if t + 1 < PACK:
                layer1(t + 1, 0, S, len(PLANE0_PIECES) + t, True)
            else:
                w3_bf = keep.tile([P, N * PACK], BF16, name="w3_bf", tag=f"scale{PACK - 1}", align_bytes=ALIGN)
                nc.vector.tensor_copy(*slots_last(w3_bf, w3_raw))
            nc.scalar.activation(nbr[t][:], h[t][:].indirect(pos_t[0][:]), ACT.Copy)
            nc.scalar.activation(own[:, t, :], h[t][:].indirect(cen_t[:]), ACT.Copy)
            nc.vector.tensor_tensor(z_sum[:, t, :], h[t][:].indirect(pos_t[1][:]), nbr[t][:], ALU.add)
        w3_mx = quantize("w3", w3_bf[:])

        def interleaved(bf, planes, u):
            return (
                bf[:, u * HALF * PACK : (u + 1) * HALF * PACK].rearrange("p (c i t) -> p c t i", i=RUN, t=PACK),
                planes[:, :, u * HALF : (u + 1) * HALF].rearrange("p t (c i) -> p c t i", i=RUN),
            )

        for u in range(2):
            nc.vector.tensor_scalar(*interleaved(z_bf, z_sum, u), 0.5, None, ALU.mult)
            nc.scalar.copy(*interleaved(own_bf, own, u))

        acc_out = [psum.tile([P, HALF], F32, name=f"acc_out{u}") for u in range(2)]

        def layer2(u, weights, values, opens):
            nc.tensor.matmul_mx(
                out=acc_out[u][:],
                lhsT=weights[0][:].bitcast(FP8X4),
                lhsT_scale=weights[1][:],
                rhs=values[0][:].bitcast(FP8X4),
                rhs_scale=values[1][:],
                start=opens,
                stop=not opens,
            )

        groups = [slice(u * HALF * PACK, (u + 1) * HALF * PACK) for u in range(2)]
        for u in range(2):
            layer2(u, w3_mx, quantize(f"z{u}", z_bf[:, groups[u]]), True)
        for u in range(2):
            layer2(u, w2_mx, quantize(f"own{u}", own_bf[:, groups[u]]), False)
            res = keep.tile([P, HALF], F32, name=f"res{u}")
            nc.scalar.copy(res[:], acc_out[u][:])
            nc.sync.dma_start(out[:, u * HALF : (u + 1) * HALF], res[:])
